import numpy as np
import ml_dtypes


def mxq(x, axis, fmt="e4m3"):
    dtype, down = {"e4m3": (ml_dtypes.float8_e4m3fn, 7), "e5m2": (ml_dtypes.float8_e5m2, 14)}[fmt]
    v = np.moveaxis(np.asarray(x, np.float32).astype(ml_dtypes.bfloat16).astype(np.float64), axis, -1)
    blocks = v.reshape(v.shape[:-1] + (-1, 32))
    amax = np.abs(blocks).max(-1, keepdims=True)
    byte = np.maximum(np.where(amax > 0, np.frexp(amax)[1] - 1 + 127, 0) - down, 1)
    scale = np.exp2(byte - 127.0)
    codes = (blocks / scale).astype(np.float32).astype(dtype).astype(np.float64)
    return np.moveaxis((codes * scale).reshape(v.shape), -1, axis)


WIDE = False


def mx_kscale(k):
    if not WIDE:
        return np.ones(k)
    levels = np.array([10, -10, 5, -5, 0])
    if k % 512:
        return np.exp2(np.random.permutation(np.resize(levels, k // 32))).repeat(32)
    a = np.empty((k // 512, 16))
    for p in range(k // 512):
        a[p, :8] = np.random.permutation(np.resize(levels, 8))
        for g in range(8):
            far = levels[np.abs(levels - a[p, g]) >= 10]
            a[p, g + 8] = far[np.random.randint(len(far))]
    return np.exp2(a.ravel()).repeat(32)


def f64(x):
    return np.asarray(x).astype(np.float64)


def striped(idx):
    return np.tile(idx.reshape(-1, 16).T, (8, 1)).astype(np.uint16)


def unstriped(offs):
    return offs[:16].T.reshape(-1).astype(np.int64)


def pack_weight(w):
    k, n = w.shape
    w = f64(np.asarray(w, np.float32).astype(ml_dtypes.bfloat16)).reshape(k // 32, 32, n)
    amax = np.abs(w).max(1)
    byte = np.clip(np.where(amax > 0, np.frexp(amax)[1] - 1 + 127 - 7, 1), 1, 254)
    scaled = (w * np.exp2(127.0 - byte)[:, None, :]).reshape(k, n).astype(np.float32)
    words = np.ascontiguousarray(scaled.reshape(k // 512, 128, 4, n).transpose(0, 1, 3, 2)).astype(ml_dtypes.float8_e4m3fn).view(np.uint8)
    return words, np.ascontiguousarray(byte.astype(np.uint8).reshape(k // 512, 16, n))


def unpack_weight(words, scales):
    g, p, n, _ = words.shape
    vals = np.ascontiguousarray(words).view(ml_dtypes.float8_e4m3fn).astype(np.float64) * np.repeat(np.exp2(scales.astype(np.float64) - 127.0), 8, axis=1)[..., None]
    return vals.transpose(0, 1, 3, 2).reshape(g * 512, n)


def planes(y):
    n, m = y.shape
    v = y.astype(np.float32).astype(ml_dtypes.bfloat16).astype(np.float64).reshape(n // 32, 32, m)
    top = np.abs(v).max(1)
    byte = np.clip(np.where(top > 0, np.frexp(top)[1] - 1 + 127 - 7, 1), 1, 254)
    codes = (v * np.exp2(127.0 - byte)[:, None, :]).reshape(n, m).astype(np.float32).astype(ml_dtypes.float8_e4m3fn).view(np.uint8)
    words = codes.reshape(n // 512, 128, 4, m).transpose(0, 1, 3, 2)
    return np.ascontiguousarray(words), np.ascontiguousarray(byte.astype(np.uint8).reshape(n // 512, 16, m))


def sigmoid(v):
    return 1.0 / (1.0 + np.exp(-np.maximum(v, -700.0)))


K, T, S, V, N = 1024, 1024, 512, 256, 512


def setup_inputs():
    n = np.random.standard_normal
    s = mx_kscale(K)[:, None]
    near = np.random.permutation(S)
    packed_xT = pack_weight(n((K, T)) * s)
    return {
        "x_words": packed_xT[0],
        "x_scales": packed_xT[1],
        "w0": (n((K, N)) / np.sqrt(K) / s).astype(np.float32),
        "w1": (n((K, N)) / np.sqrt(K) / s).astype(np.float32),
        "w2": (n((K, N)) / np.sqrt(K) / s).astype(np.float32),
        "w3": (n((K, N)) / np.sqrt(K) / s).astype(np.float32),
        "offs": striped(np.random.permutation(T)[:S]),
        "cen": striped(np.random.permutation(S)[:V]),
        "pos1": striped(near[:V]),
        "pos2": striped(near[V:]),
        "pos3": striped(np.random.permutation(S)[:V]),
    }


def reference(x_words, x_scales, w0, w1, w2, w3, offs, cen, pos1, pos2, pos3):
    xq = unpack_weight(x_words, x_scales)[:, unstriped(offs)]
    m0 = sigmoid(mxq(f64(w1), 0, "e4m3").T @ xq)
    c0 = m0[:, unstriped(cen)]
    y = mxq(f64(w0), 0, "e4m3").T @ xq
    m1 = sigmoid(mxq(f64(w2), 0, "e4m3").T @ xq)
    c1 = m1[:, unstriped(cen)]
    m2 = sigmoid(mxq(f64(w3), 0, "e4m3").T @ xq)
    c2 = m2[:, unstriped(cen)]
    out_0 = c0 * y[:, unstriped(pos1)] + c1 * y[:, unstriped(pos2)] + c2 * y[:, unstriped(pos3)]
    return (out_0,) + planes(out_0)

@@ -1,0 +1,181 @@
+from contextlib import ExitStack
+
+import concourse.mybir as mybir
+
+K, T, S, V, N = 1024, 1024, 512, 256, 512
+FLOPS = 4 * 2 * K * N * S
+
+F32 = mybir.dt.float32
+BF16 = mybir.dt.bfloat16
+I32 = mybir.dt.int32
+U32 = mybir.dt.uint32
+U16 = mybir.dt.uint16
+U8 = mybir.dt.uint8
+FP8X4 = mybir.dt.float8_e4m3fn_x4
+SIGMOID = mybir.ActivationFunctionType.Sigmoid
+MULT = mybir.AluOpType.mult
+
+P = 128
+PACK = 4
+K_PASS = P * PACK
+PASSES = K // K_PASS
+CAST_ON_SCALAR = ((0, 0, 0), (0, 1, 0), (1, 0, 0), (1, 1, 0), (2, 0, 0), (3, 1, 1))
+
+
+def tile_picked_zmodd_none_po_kernel(
+    tc, x_words, x_scales, w0, w1, w2, w3, offs, cen, pos1, pos2, pos3, out_0, out_1, out_2
+):
+    nc = tc.nc
+    weights = (w0, w1, w2, w3)
+    with ExitStack() as ctx:
+        keep = ctx.enter_context(tc.tile_pool(name="keep", bufs=1))
+        psum = ctx.enter_context(tc.psum_pool(name="psum", bufs=8))
+
+        def load_list(src, name):
+            tile = keep.tile([P, src.shape[1]], U16, name=name)
+            nc.sync.dma_start(tile[:], src)
+            return tile
+
+        def load_weight(w, g):
+            raw = keep.tile([P, PACK, N], F32, name="raw%d_%d" % (w, g))
+            rows = weights[w][g * K_PASS : (g + 1) * K_PASS, :]
+            nc.sync.dma_start(out=raw[:], in_=rows.rearrange("(p j) c -> p j c", j=PACK))
+            return raw
+
+        warm_in = keep.tile([P, 1], F32, name="warm_in")
+        warm_out = keep.tile([P, 1], F32, name="warm_out")
+        nc.gpsimd.memset(warm_in[:], 0.0)
+        nc.scalar.activation(warm_out[:], warm_in[:], SIGMOID)
+
+        x_planes = keep.tile([P, T], U8, name="x_planes", align_bytes=64)
+        nc.vector.memset(x_planes[:].bitcast(I32), 0)
+        offs_t = load_list(offs, "offs_t")
+        x_table = []
+        for g in range(PASSES):
+            table = keep.tile([P, T], I32, name="x_table%d" % g, align_bytes=64)
+            nc.sync.dma_start(out=table[:], in_=x_words[g].rearrange("p c r -> p (c r)").bitcast(I32))
+            x_table.append(table)
+        for q in range(4):
+            nc.scalar.dma_start(
+                out=x_planes[32 * q : 32 * q + 4 * PASSES, :].bitcast(I32),
+                in_=x_scales[:, 4 * q : 4 * q + 4, :].bitcast(I32),
+            )
+        raw = {}
+        raw[0, 0] = load_weight(0, 0)
+        raw[0, 1] = load_weight(0, 1)
+        raw[1, 0] = load_weight(1, 0)
+        cen_t = load_list(cen, "cen_t")
+        pos_t = [load_list(pos1, "pos1_t")]
+        raw[1, 1] = load_weight(1, 1)
+        pos_t.append(load_list(pos3, "pos3_t"))
+        raw[2, 0] = load_weight(2, 0)
+        pos_t.insert(1, load_list(pos2, "pos2_t"))
+        raw[2, 1] = load_weight(2, 1)
+        raw[3, 0] = load_weight(3, 0)
+        raw[3, 1] = load_weight(3, 1)
+
+        x_codes = []
+        for g in range(PASSES):
+            picked = keep.tile([P, S], U32, name="x_codes%d" % g, align_bytes=64)
+            nc.vector.tensor_copy(picked[:], x_table[g][:].bitcast(U32).indirect(offs_t[:]))
+            x_codes.append(picked)
+        x_bytes = keep.tile([P, S], U8, name="x_bytes", align_bytes=64)
+        nc.vector.tensor_copy(x_bytes[:], x_planes[:].indirect(offs_t[:]))
+
+        def round_weight(w, g, h):
+            dealt = keep.tile([P, 2, P, PACK], BF16, name="dealt%d_%d_%d" % (w, g, h), align_bytes=64)
+            src = raw[w, g][:].rearrange("p j (m h t) -> p h m j t", h=2, t=2)[:, h]
+            dst = dealt[:].rearrange("p t m j -> p m j t")
+            if (w, g, h) in CAST_ON_SCALAR:
+                nc.scalar.copy(dst, src)
+            else:
+                nc.vector.tensor_copy(dst, src)
+            return dealt
+
+        def quantize_weight(dealt, w, g, h):
+            codes = keep.tile([P, 2 * P], U32, name="codes%d_%d_%d" % (w, g, h), align_bytes=64)
+            scales = keep.tile([P, 2 * P], U8, name="scales%d_%d_%d" % (w, g, h), align_bytes=64)
+            nc.vector.quantize_mx(
+                out=codes[:].bitcast(FP8X4), scales=scales[:], in_=dealt[:].rearrange("p t m j -> p (t m j)")
+            )
+            return codes, scales
+
+        def product(w):
+            banks = [psum.tile([P, S], F32, name="bank") for t in range(PACK)]
+            for g in range(PASSES):
+                dealt = [round_weight(w, g, h) for h in range(2)]
+                for h in range(2):
+                    codes, scales = quantize_weight(dealt[h], w, g, h)
+                    for t in range(2):
+                        cols = slice(t * P, (t + 1) * P)
+                        nc.tensor.matmul_mx(
+                            out=banks[2 * h + t][:],
+                            lhsT=codes[:, cols].bitcast(FP8X4),
+                            lhsT_scale=scales[:, cols],
+                            rhs=x_codes[g][:].bitcast(FP8X4),
+                            rhs_scale=x_bytes[4 * g :, :],
+                            start=(g == 0),
+                            stop=(g == PASSES - 1),
+                        )
+            return banks
+
+        def rows_tile(name, width):
+            return keep.tile([P, width], F32, name=name)
+
+        y_banks = product(0)
+        mask_banks = product(1)
+        y = []
+        for t in range(PACK):
+            y.append(rows_tile("y%d" % t, S))
+            nc.scalar.copy(y[t][:], y_banks[t][:])
+
+        def tap(d, banks):
+            terms = []
+            for t in range(PACK):
+                sums = rows_tile("sums%d_%d" % (d, t), S)
+                nc.scalar.copy(sums[:], banks[t][:])
+                mask = rows_tile("mask%d_%d" % (d, t), V)
+                nc.scalar.activation(mask[:], sums[:].indirect(cen_t[:]), SIGMOID)
+                term = rows_tile("term%d_%d" % (d, t), V)
+                nc.vector.tensor_tensor(term[:], y[t][:].indirect(pos_t[d][:]), mask[:], MULT)
+                terms.append(term)
+            return terms
+
+        next_banks = product(2)
+        term0 = tap(0, mask_banks)
+        last_banks = product(3)
+        term1 = tap(1, next_banks)
+        partial = []
+        sampled = []
+        for t in range(PACK):
+            partial.append(rows_tile("partial%d" % t, V))
+            nc.vector.tensor_add(partial[t][:], term0[t][:], term1[t][:])
+            sampled.append(rows_tile("sampled%d" % t, V))
+            nc.vector.tensor_copy(sampled[t][:], y[t][:].indirect(pos_t[2][:]))
+
+        result = keep.tile([P, PACK, V], F32, name="result")
+        out_rows = out_0.rearrange("(p t) v -> p t v", t=PACK)
+        for t in range(PACK):
+            mask = rows_tile("mask2_%d" % t, S)
+            nc.scalar.activation(mask[:], last_banks[t][:], SIGMOID)
+            term = rows_tile("term2_%d" % t, V)
+            nc.vector.tensor_tensor(term[:], mask[:].indirect(cen_t[:]), sampled[t][:], MULT)
+            nc.vector.tensor_add(result[:, t, :], partial[t][:], term[:])
+            nc.sync.dma_start(out=out_rows[:, t, :], in_=result[:, t, :])
+
+        rounded = keep.tile([P, V, PACK], BF16, name="rounded", align_bytes=64)
+        nc.vector.tensor_copy(
+            rounded[:].rearrange("p (c i) t -> p c t i", i=4),
+            result[:].rearrange("p t (c i) -> p c t i", i=4),
+        )
+        out_codes = keep.tile([P, V], U32, name="out_codes", align_bytes=64)
+        out_scales = keep.tile([P, V], U8, name="out_scales", align_bytes=64)
+        nc.vector.quantize_mx(
+            out=out_codes[:].bitcast(FP8X4), scales=out_scales[:], in_=rounded[:].rearrange("p v t -> p (v t)")
+        )
+        nc.sync.dma_start(out=out_1[0].rearrange("p c r -> p (c r)").bitcast(I32), in_=out_codes[:].bitcast(I32))
+        for q in range(4):
+            queue = nc.scalar if q % 2 else nc.sync
+            queue.dma_start(
+                out=out_2[0, 4 * q : 4 * q + 4, :].bitcast(I32), in_=out_scales[32 * q : 32 * q + 4, :].bitcast(I32)
+            )

@@ -19,7 +19,7 @@ P = 128
 PACK = 4
 K_PASS = P * PACK
 PASSES = K // K_PASS
-CAST_ON_SCALAR = ((0, 0, 0), (0, 1, 0), (1, 0, 0), (1, 1, 0), (2, 0, 0), (3, 1, 1))
+CAST_ON_SCALAR = ((1, 0, 0), (1, 1, 0), (2, 1, 0), (2, 1, 1))
 
 
 def tile_picked_zmodd_none_po_kernel(
@@ -42,13 +42,13 @@ def tile_picked_zmodd_none_po_kernel(
             nc.sync.dma_start(out=raw[:], in_=rows.rearrange("(p j) c -> p j c", j=PACK))
             return raw
 
-        warm_in = keep.tile([P, 1], F32, name="warm_in")
-        warm_out = keep.tile([P, 1], F32, name="warm_out")
-        nc.gpsimd.memset(warm_in[:], 0.0)
-        nc.scalar.activation(warm_out[:], warm_in[:], SIGMOID)
-
         x_planes = keep.tile([P, T], U8, name="x_planes", align_bytes=64)
         nc.vector.memset(x_planes[:].bitcast(I32), 0)
+        warm_in = keep.tile([P, 1], F32, name="warm_in")
+        warm_out = keep.tile([P, 1], F32, name="warm_out")
+        nc.vector.memset(warm_in[:], 0.0)
+        nc.scalar.activation(warm_out[:], warm_in[:], SIGMOID)
+
         offs_t = load_list(offs, "offs_t")
         x_table = []
         for g in range(PASSES):
@@ -56,21 +56,21 @@ def tile_picked_zmodd_none_po_kernel(
             nc.sync.dma_start(out=table[:], in_=x_words[g].rearrange("p c r -> p (c r)").bitcast(I32))
             x_table.append(table)
         for q in range(4):
-            nc.scalar.dma_start(
+            nc.sync.dma_start(
                 out=x_planes[32 * q : 32 * q + 4 * PASSES, :].bitcast(I32),
                 in_=x_scales[:, 4 * q : 4 * q + 4, :].bitcast(I32),
             )
         raw = {}
+        raw[1, 0] = load_weight(1, 0)
+        raw[1, 1] = load_weight(1, 1)
+        cen_t = load_list(cen, "cen_t")
         raw[0, 0] = load_weight(0, 0)
         raw[0, 1] = load_weight(0, 1)
-        raw[1, 0] = load_weight(1, 0)
-        cen_t = load_list(cen, "cen_t")
         pos_t = [load_list(pos1, "pos1_t")]
-        raw[1, 1] = load_weight(1, 1)
-        pos_t.append(load_list(pos3, "pos3_t"))
         raw[2, 0] = load_weight(2, 0)
-        pos_t.insert(1, load_list(pos2, "pos2_t"))
+        pos_t.append(load_list(pos2, "pos2_t"))
         raw[2, 1] = load_weight(2, 1)
+        pos_t.append(load_list(pos3, "pos3_t"))
         raw[3, 0] = load_weight(3, 0)
         raw[3, 1] = load_weight(3, 1)
 
@@ -82,92 +82,90 @@ def tile_picked_zmodd_none_po_kernel(
         x_bytes = keep.tile([P, S], U8, name="x_bytes", align_bytes=64)
         nc.vector.tensor_copy(x_bytes[:], x_planes[:].indirect(offs_t[:]))
 
-        def round_weight(w, g, h):
-            dealt = keep.tile([P, 2, P, PACK], BF16, name="dealt%d_%d_%d" % (w, g, h), align_bytes=64)
-            src = raw[w, g][:].rearrange("p j (m h t) -> p h m j t", h=2, t=2)[:, h]
-            dst = dealt[:].rearrange("p t m j -> p m j t")
-            if (w, g, h) in CAST_ON_SCALAR:
-                nc.scalar.copy(dst, src)
-            else:
-                nc.vector.tensor_copy(dst, src)
-            return dealt
-
-        def quantize_weight(dealt, w, g, h):
-            codes = keep.tile([P, 2 * P], U32, name="codes%d_%d_%d" % (w, g, h), align_bytes=64)
-            scales = keep.tile([P, 2 * P], U8, name="scales%d_%d_%d" % (w, g, h), align_bytes=64)
-            nc.vector.quantize_mx(
-                out=codes[:].bitcast(FP8X4), scales=scales[:], in_=dealt[:].rearrange("p t m j -> p (t m j)")
-            )
-            return codes, scales
 
         def product(w):
             banks = [psum.tile([P, S], F32, name="bank") for t in range(PACK)]
             for g in range(PASSES):
-                dealt = [round_weight(w, g, h) for h in range(2)]
+                dealt = keep.tile([P, PACK, P, PACK], BF16, name="dealt%d_%d" % (w, g), tag="dealt%d_%d" % (w, g), align_bytes=64)
                 for h in range(2):
-                    codes, scales = quantize_weight(dealt[h], w, g, h)
-                    for t in range(2):
-                        cols = slice(t * P, (t + 1) * P)
-                        nc.tensor.matmul_mx(
-                            out=banks[2 * h + t][:],
-                            lhsT=codes[:, cols].bitcast(FP8X4),
-                            lhsT_scale=scales[:, cols],
-                            rhs=x_codes[g][:].bitcast(FP8X4),
-                            rhs_scale=x_bytes[4 * g :, :],
-                            start=(g == 0),
-                            stop=(g == PASSES - 1),
-                        )
+                    src = raw[w, g][:].rearrange("p j (m h t) -> p h m j t", h=2, t=2)[:, h]
+                    dst = dealt[:, 2 * h : 2 * h + 2].rearrange("p t m j -> p m j t")
+                    if (w, g, h) in CAST_ON_SCALAR:
+                        nc.scalar.copy(dst, src)
+                    else:
+                        nc.vector.tensor_copy(dst, src)
+                codes = keep.tile([P, N], U32, name="codes%d_%d" % (w, g), align_bytes=64)
+                scales = keep.tile([P, N], U8, name="scales%d_%d" % (w, g), align_bytes=64)
+                flat = dealt[:].rearrange("p t m j -> p (t m j)")
+                parts = 2
+                width = N // parts
+                for part in range(parts):
+                    cols = slice(part * width, (part + 1) * width)
+                    nc.vector.quantize_mx(
+                        out=codes[:, cols].bitcast(FP8X4),
+                        scales=scales[:, cols],
+                        in_=flat[:, PACK * part * width : PACK * (part + 1) * width],
+                    )
+
+                for t in range(PACK):
+                    cols = slice(t * P, (t + 1) * P)
+                    nc.tensor.matmul_mx(
+                        out=banks[t][:],
+                        lhsT=codes[:, cols].bitcast(FP8X4),
+                        lhsT_scale=scales[:, cols],
+                        rhs=x_codes[g][:].bitcast(FP8X4),
+                        rhs_scale=x_bytes[4 * g :, :],
+                        start=(g == 0),
+                        stop=(g == PASSES - 1),
+                    )
             return banks
 
         def rows_tile(name, width):
             return keep.tile([P, width], F32, name=name)
 
+        def picked_mask(d, t, bank):
+            sums = rows_tile("sums%d_%d" % (d, t), S)
+            nc.scalar.copy(sums[:], bank[:])
+            mask = rows_tile("mask%d_%d" % (d, t), V)
+            nc.scalar.activation(mask[:], sums[:].indirect(cen_t[:]), SIGMOID)
+            return mask
+
+        terms = []
+        y = [rows_tile("y%d" % t, S) for t in range(PACK)]
+
+        def term(d, t, mask):
+            nc.vector.tensor_tensor(terms[d][:, t, :], y[t][:].indirect(pos_t[d][:]), mask[:], MULT)
+
+        banks0 = product(1)
         y_banks = product(0)
-        mask_banks = product(1)
-        y = []
+        masks0 = [picked_mask(0, t, banks0[t]) for t in range(PACK)]
+        banks1 = product(2)
         for t in range(PACK):
-            y.append(rows_tile("y%d" % t, S))
-            nc.scalar.copy(y[t][:], y_banks[t][:])
-
-        def tap(d, banks):
-            terms = []
-            for t in range(PACK):
-                sums = rows_tile("sums%d_%d" % (d, t), S)
-                nc.scalar.copy(sums[:], banks[t][:])
-                mask = rows_tile("mask%d_%d" % (d, t), V)
-                nc.scalar.activation(mask[:], sums[:].indirect(cen_t[:]), SIGMOID)
-                term = rows_tile("term%d_%d" % (d, t), V)
-                nc.vector.tensor_tensor(term[:], y[t][:].indirect(pos_t[d][:]), mask[:], MULT)
-                terms.append(term)
-            return terms
-
-        next_banks = product(2)
-        term0 = tap(0, mask_banks)
-        last_banks = product(3)
-        term1 = tap(1, next_banks)
-        partial = []
-        sampled = []
+            if t in ():
+                nc.vector.tensor_copy(y[t][:], y_banks[t][:])
+            else:
+                nc.scalar.copy(y[t][:], y_banks[t][:])
+        terms.append(keep.tile([P, PACK, V], F32, name="terms0", tag="dealt2_0", align_bytes=64))
         for t in range(PACK):
-            partial.append(rows_tile("partial%d" % t, V))
-            nc.vector.tensor_add(partial[t][:], term0[t][:], term1[t][:])
-            sampled.append(rows_tile("sampled%d" % t, V))
-            nc.vector.tensor_copy(sampled[t][:], y[t][:].indirect(pos_t[2][:]))
+            term(0, t, masks0[t])
+        banks2 = product(3)
+        terms.append(keep.tile([P, PACK, V], F32, name="terms1", tag="dealt3_1", align_bytes=64))
+        terms.append(keep.tile([P, PACK, V], F32, name="terms2"))
+        for t in range(PACK):
+            term(1, t, picked_mask(1, t, banks1[t]))
+        partial = keep.tile([P, PACK, V], F32, name="partial")
+        nc.vector.tensor_add(partial[:], terms[0][:], terms[1][:])
 
         result = keep.tile([P, PACK, V], F32, name="result")
         out_rows = out_0.rearrange("(p t) v -> p t v", t=PACK)
         for t in range(PACK):
-            mask = rows_tile("mask2_%d" % t, S)
-            nc.scalar.activation(mask[:], last_banks[t][:], SIGMOID)
-            term = rows_tile("term2_%d" % t, V)
-            nc.vector.tensor_tensor(term[:], mask[:].indirect(cen_t[:]), sampled[t][:], MULT)
-            nc.vector.tensor_add(result[:, t, :], partial[t][:], term[:])
+            term(2, t, picked_mask(2, t, banks2[t]))
+            nc.vector.tensor_add(result[:, t, :], partial[:, t, :], terms[2][:, t, :])
             nc.sync.dma_start(out=out_rows[:, t, :], in_=result[:, t, :])
 
         rounded = keep.tile([P, V, PACK], BF16, name="rounded", align_bytes=64)
-        nc.vector.tensor_copy(
-            rounded[:].rearrange("p (c i) t -> p c t i", i=4),
-            result[:].rearrange("p t (c i) -> p c t i", i=4),
-        )
+        nc.scalar.copy(rounded[:, :, 0:2], result[:, 0:2, :].rearrange("p t v -> p v t"))
+        nc.vector.tensor_copy(rounded[:, :, 2:4], result[:, 2:4, :].rearrange("p t v -> p v t"))
         out_codes = keep.tile([P, V], U32, name="out_codes", align_bytes=64)
         out_scales = keep.tile([P, V], U8, name="out_scales", align_bytes=64)
         nc.vector.quantize_mx(

@@ -19,7 +19,7 @@ P = 128
 PACK = 4
 K_PASS = P * PACK
 PASSES = K // K_PASS
-CAST_ON_SCALAR = ((1, 0, 0), (1, 1, 0), (2, 1, 0), (2, 1, 1))
+CAST_ON_SCALAR = ((2, 1, 0), (2, 1, 1))
 
 
 def tile_picked_zmodd_none_po_kernel(
@@ -44,11 +44,6 @@ def tile_picked_zmodd_none_po_kernel(
 
         x_planes = keep.tile([P, T], U8, name="x_planes", align_bytes=64)
         nc.vector.memset(x_planes[:].bitcast(I32), 0)
-        warm_in = keep.tile([P, 1], F32, name="warm_in")
-        warm_out = keep.tile([P, 1], F32, name="warm_out")
-        nc.vector.memset(warm_in[:], 0.0)
-        nc.scalar.activation(warm_out[:], warm_in[:], SIGMOID)
-
         offs_t = load_list(offs, "offs_t")
         x_table = []
         for g in range(PASSES):
@@ -125,9 +120,13 @@ def tile_picked_zmodd_none_po_kernel(
 
         def picked_mask(d, t, bank):
             sums = rows_tile("sums%d_%d" % (d, t), S)
-            nc.scalar.copy(sums[:], bank[:])
             mask = rows_tile("mask%d_%d" % (d, t), V)
-            nc.scalar.activation(mask[:], sums[:].indirect(cen_t[:]), SIGMOID)
+            if (d, t) == (0, 0):
+                nc.scalar.activation(sums[:], bank[:], SIGMOID)
+                nc.vector.tensor_copy(mask[:], sums[:].indirect(cen_t[:]))
+            else:
+                nc.scalar.copy(sums[:], bank[:])
+                nc.scalar.activation(mask[:], sums[:].indirect(cen_t[:]), SIGMOID)
             return mask
 
         terms = []

@@ -19,7 +19,6 @@ P = 128
 PACK = 4
 K_PASS = P * PACK
 PASSES = K // K_PASS
-CAST_ON_SCALAR = ((2, 1, 0), (2, 1, 1))
 
 
 def tile_picked_zmodd_none_po_kernel(
@@ -27,146 +26,168 @@ def tile_picked_zmodd_none_po_kernel(
 ):
     nc = tc.nc
     weights = (w0, w1, w2, w3)
+    vector, scalar = nc.vector.tensor_copy, nc.scalar.copy
     with ExitStack() as ctx:
         keep = ctx.enter_context(tc.tile_pool(name="keep", bufs=1))
         psum = ctx.enter_context(tc.psum_pool(name="psum", bufs=8))
 
+        def tile(shape, dtype, name, tag=None):
+            return keep.tile(shape, dtype, name=name, tag=tag or name, align_bytes=64)
+
         def load_list(src, name):
-            tile = keep.tile([P, src.shape[1]], U16, name=name)
-            nc.sync.dma_start(tile[:], src)
-            return tile
+            offsets = keep.tile([P, src.shape[1]], U16, name=name)
+            nc.sync.dma_start(offsets[:], src)
+            return offsets
 
-        def load_weight(w, g):
-            raw = keep.tile([P, PACK, N], F32, name="raw%d_%d" % (w, g))
-            rows = weights[w][g * K_PASS : (g + 1) * K_PASS, :]
-            nc.sync.dma_start(out=raw[:], in_=rows.rearrange("(p j) c -> p j c", j=PACK))
-            return raw
+        raw = {}
 
-        x_planes = keep.tile([P, T], U8, name="x_planes", align_bytes=64)
+        def load_weight(w, g, *cuts):
+            edges = (0,) + cuts + (N,)
+            raw[w, g] = []
+            for first, last in zip(edges, edges[1:]):
+                piece = tile([P, PACK, last - first], F32, "raw%d_%d_%d" % (w, g, first))
+                rows = weights[w][g * K_PASS : (g + 1) * K_PASS, first:last]
+                nc.sync.dma_start(out=piece[:], in_=rows.rearrange("(p j) c -> p j c", j=PACK))
+                raw[w, g].append((piece, slice(first // PACK, last // PACK)))
+
+        def load_words(g):
+            table = tile([P, T], I32, "x_table%d" % g)
+            nc.sync.dma_start(out=table[:], in_=x_words[g].rearrange("p c r -> p (c r)").bitcast(I32))
+            return table
+
+        def load_scales():
+            for q in range(4):
+                nc.sync.dma_start(
+                    out=x_planes[32 * q : 32 * q + 4 * PASSES, :].bitcast(I32),
+                    in_=x_scales[:, 4 * q : 4 * q + 4, :].bitcast(I32),
+                )
+
+        warm = tile([P, 2], F32, "warm")
+        nc.gpsimd.memset(warm[:, 0:1], 0.0)
+        nc.scalar.activation(warm[:, 1:2], warm[:, 0:1], SIGMOID)
+
+        x_planes = tile([P, T], U8, "x_planes")
         nc.vector.memset(x_planes[:].bitcast(I32), 0)
         offs_t = load_list(offs, "offs_t")
-        x_table = []
-        for g in range(PASSES):
-            table = keep.tile([P, T], I32, name="x_table%d" % g, align_bytes=64)
-            nc.sync.dma_start(out=table[:], in_=x_words[g].rearrange("p c r -> p (c r)").bitcast(I32))
-            x_table.append(table)
-        for q in range(4):
-            nc.sync.dma_start(
-                out=x_planes[32 * q : 32 * q + 4 * PASSES, :].bitcast(I32),
-                in_=x_scales[:, 4 * q : 4 * q + 4, :].bitcast(I32),
-            )
-        raw = {}
-        raw[1, 0] = load_weight(1, 0)
-        raw[1, 1] = load_weight(1, 1)
+        x_table = [load_words(0)]
+        x_table.append(load_words(1))
+        load_scales()
+        load_weight(1, 0)
+        load_weight(1, 1, 384)
         cen_t = load_list(cen, "cen_t")
-        raw[0, 0] = load_weight(0, 0)
-        raw[0, 1] = load_weight(0, 1)
+        load_weight(0, 0, 256)
+        load_weight(0, 1, 384)
         pos_t = [load_list(pos1, "pos1_t")]
-        raw[2, 0] = load_weight(2, 0)
+        load_weight(2, 0, 256)
         pos_t.append(load_list(pos2, "pos2_t"))
-        raw[2, 1] = load_weight(2, 1)
+        load_weight(2, 1)
         pos_t.append(load_list(pos3, "pos3_t"))
-        raw[3, 0] = load_weight(3, 0)
-        raw[3, 1] = load_weight(3, 1)
+        load_weight(3, 0)
+        load_weight(3, 1)
 
-        x_codes = []
-        for g in range(PASSES):
-            picked = keep.tile([P, S], U32, name="x_codes%d" % g, align_bytes=64)
-            nc.vector.tensor_copy(picked[:], x_table[g][:].bitcast(U32).indirect(offs_t[:]))
-            x_codes.append(picked)
-        x_bytes = keep.tile([P, S], U8, name="x_bytes", align_bytes=64)
-        nc.vector.tensor_copy(x_bytes[:], x_planes[:].indirect(offs_t[:]))
+        x_codes = [tile([P, S], U32, "x_codes%d" % g) for g in range(PASSES)]
+        x_bytes = tile([P, S], U8, "x_bytes")
 
+        def pick_words(g):
+            nc.vector.tensor_copy(x_codes[g][:], x_table[g][:].bitcast(U32).indirect(offs_t[:]))
 
-        def product(w):
-            banks = [psum.tile([P, S], F32, name="bank") for t in range(PACK)]
-            for g in range(PASSES):
-                dealt = keep.tile([P, PACK, P, PACK], BF16, name="dealt%d_%d" % (w, g), tag="dealt%d_%d" % (w, g), align_bytes=64)
+        def pick_bytes():
+            nc.vector.tensor_copy(x_bytes[:], x_planes[:].indirect(offs_t[:]))
+
+        dealt, banks, rows, picked, terms = {}, {}, {}, {}, {}
+
+        def deal(w, g, copies):
+            for h in range(2):
+                dealt[w, g, h] = tile([P, 2, P, PACK], BF16, "dealt%d_%d_%d" % (w, g, h))
+            for piece, span in raw[w, g]:
                 for h in range(2):
-                    src = raw[w, g][:].rearrange("p j (m h t) -> p h m j t", h=2, t=2)[:, h]
-                    dst = dealt[:, 2 * h : 2 * h + 2].rearrange("p t m j -> p m j t")
-                    if (w, g, h) in CAST_ON_SCALAR:
-                        nc.scalar.copy(dst, src)
-                    else:
-                        nc.vector.tensor_copy(dst, src)
-                codes = keep.tile([P, N], U32, name="codes%d_%d" % (w, g), align_bytes=64)
-                scales = keep.tile([P, N], U8, name="scales%d_%d" % (w, g), align_bytes=64)
-                flat = dealt[:].rearrange("p t m j -> p (t m j)")
-                parts = 2
-                width = N // parts
-                for part in range(parts):
-                    cols = slice(part * width, (part + 1) * width)
-                    nc.vector.quantize_mx(
-                        out=codes[:, cols].bitcast(FP8X4),
-                        scales=scales[:, cols],
-                        in_=flat[:, PACK * part * width : PACK * (part + 1) * width],
-                    )
+                    src = piece[:].rearrange("p j (m h t) -> p h m j t", h=2, t=2)[:, h]
+                    copies[h](dealt[w, g, h][:, :, span].rearrange("p t m j -> p m j t"), src)
 
-                for t in range(PACK):
-                    cols = slice(t * P, (t + 1) * P)
-                    nc.tensor.matmul_mx(
-                        out=banks[t][:],
-                        lhsT=codes[:, cols].bitcast(FP8X4),
-                        lhsT_scale=scales[:, cols],
-                        rhs=x_codes[g][:].bitcast(FP8X4),
-                        rhs_scale=x_bytes[4 * g :, :],
-                        start=(g == 0),
-                        stop=(g == PASSES - 1),
-                    )
-            return banks
+        def multiply(w, g, h, tag=None):
+            codes = tile([P, 2 * P], U32, "codes%d_%d_%d" % (w, g, h), tag)
+            scales = tile([P, 2 * P], U8, "scales%d_%d_%d" % (w, g, h))
+            nc.vector.quantize_mx(
+                out=codes[:].bitcast(FP8X4), scales=scales[:], in_=dealt[w, g, h][:].rearrange("p t m j -> p (t m j)")
+            )
+            for s in range(2):
+                t = 2 * h + s
+                if g == 0:
+                    banks[w, t] = psum.tile([P, S], F32, name="bank")
+                cols = slice(s * P, (s + 1) * P)
+                nc.tensor.matmul_mx(
+                    out=banks[w, t][:],
+                    lhsT=codes[:, cols].bitcast(FP8X4),
+                    lhsT_scale=scales[:, cols],
+                    rhs=x_codes[g][:].bitcast(FP8X4),
+                    rhs_scale=x_bytes[4 * g :, :],
+                    start=(g == 0),
+                    stop=(g == PASSES - 1),
+                )
 
-        def rows_tile(name, width):
-            return keep.tile([P, width], F32, name=name)
+        def whole_pass(w, g, first=vector, second=vector):
+            deal(w, g, (first, second))
+            multiply(w, g, 0)
+            multiply(w, g, 1)
 
-        def picked_mask(d, t, bank):
-            sums = rows_tile("sums%d_%d" % (d, t), S)
-            mask = rows_tile("mask%d_%d" % (d, t), V)
-            if (d, t) == (0, 0):
-                nc.scalar.activation(sums[:], bank[:], SIGMOID)
-                nc.vector.tensor_copy(mask[:], sums[:].indirect(cen_t[:]))
-            else:
-                nc.scalar.copy(sums[:], bank[:])
-                nc.scalar.activation(mask[:], sums[:].indirect(cen_t[:]), SIGMOID)
-            return mask
+        def empty(w, t, copy=scalar, tag=None):
+            rows[w, t] = tile([P, S], F32, "rows%d_%d" % (w, t), tag)
+            copy(rows[w, t][:], banks[w, t][:])
 
-        terms = []
-        y = [rows_tile("y%d" % t, S) for t in range(PACK)]
+        def pick(w, t, tag=None):
+            picked[w, t] = tile([P, V], F32, "mask%d_%d" % (w, t), tag)
+            nc.scalar.activation(picked[w, t][:], rows[w, t][:].indirect(cen_t[:]), SIGMOID)
 
-        def term(d, t, mask):
-            nc.vector.tensor_tensor(terms[d][:, t, :], y[t][:].indirect(pos_t[d][:]), mask[:], MULT)
+        def term(w, t, out):
+            nc.vector.tensor_tensor(out, rows[0, t][:].indirect(pos_t[w - 1][:]), picked[w, t][:], MULT)
 
-        banks0 = product(1)
-        y_banks = product(0)
-        masks0 = [picked_mask(0, t, banks0[t]) for t in range(PACK)]
-        banks1 = product(2)
+        pick_words(0)
+        pick_words(1)
+        pick_bytes()
+        whole_pass(1, 0, vector, scalar)
+        whole_pass(1, 1, vector, scalar)
+        whole_pass(0, 0)
+        whole_pass(0, 1)
         for t in range(PACK):
-            if t in ():
-                nc.vector.tensor_copy(y[t][:], y_banks[t][:])
-            else:
-                nc.scalar.copy(y[t][:], y_banks[t][:])
-        terms.append(keep.tile([P, PACK, V], F32, name="terms0", tag="dealt2_0", align_bytes=64))
+            empty(1, t)
+            pick(1, t)
+        whole_pass(2, 0)
         for t in range(PACK):
-            term(0, t, masks0[t])
-        banks2 = product(3)
-        terms.append(keep.tile([P, PACK, V], F32, name="terms1", tag="dealt3_1", align_bytes=64))
-        terms.append(keep.tile([P, PACK, V], F32, name="terms2"))
+            empty(0, t)
+        deal(2, 1, (scalar, scalar))
+        early = tile([P, PACK - 1, V], F32, "early", "dealt2_0_0")
+        for t in range(PACK - 1):
+            term(1, t, early[:, t, :])
+        multiply(2, 1, 0)
+        fourth = tile([P, V], F32, "fourth", "dealt2_1_0")
+        term(1, PACK - 1, fourth[:])
+        multiply(2, 1, 1)
+        whole_pass(3, 0, vector, scalar)
+        whole_pass(3, 1)
         for t in range(PACK):
-            term(1, t, picked_mask(1, t, banks1[t]))
-        partial = keep.tile([P, PACK, V], F32, name="partial")
-        nc.vector.tensor_add(partial[:], terms[0][:], terms[1][:])
-
-        result = keep.tile([P, PACK, V], F32, name="result")
+            empty(2, t)
+            pick(2, t)
+        terms1 = tile([P, PACK, V], F32, "terms1", "dealt3_1_0")
+        for t in range(PACK):
+            term(2, t, terms1[:, t, :])
+        partial = tile([P, PACK, V], F32, "partial")
+        nc.vector.tensor_add(partial[:, : PACK - 1, :], early[:], terms1[:, : PACK - 1, :])
+        nc.vector.tensor_add(partial[:, PACK - 1, :], fourth[:], terms1[:, PACK - 1, :])
+        terms2 = tile([P, PACK, V], F32, "terms2")
+        result = tile([P, PACK, V], F32, "result")
         out_rows = out_0.rearrange("(p t) v -> p t v", t=PACK)
         for t in range(PACK):
-            term(2, t, picked_mask(2, t, banks2[t]))
-            nc.vector.tensor_add(result[:, t, :], partial[:, t, :], terms[2][:, t, :])
+            empty(3, t)
+            pick(3, t)
+            term(3, t, terms2[:, t, :])
+            nc.vector.tensor_add(result[:, t, :], partial[:, t, :], terms2[:, t, :])
             nc.sync.dma_start(out=out_rows[:, t, :], in_=result[:, t, :])
 
-        rounded = keep.tile([P, V, PACK], BF16, name="rounded", align_bytes=64)
-        nc.scalar.copy(rounded[:, :, 0:2], result[:, 0:2, :].rearrange("p t v -> p v t"))
-        nc.vector.tensor_copy(rounded[:, :, 2:4], result[:, 2:4, :].rearrange("p t v -> p v t"))
-        out_codes = keep.tile([P, V], U32, name="out_codes", align_bytes=64)
-        out_scales = keep.tile([P, V], U8, name="out_scales", align_bytes=64)
+        rounded = tile([P, V, PACK], BF16, "rounded")
+        scalar(rounded[:, :, 0:2], result[:, 0:2, :].rearrange("p t v -> p v t"))
+        vector(rounded[:, :, 2:4], result[:, 2:4, :].rearrange("p t v -> p v t"))
+        out_codes = tile([P, V], U32, "out_codes")
+        out_scales = tile([P, V], U8, "out_scales")
         nc.vector.quantize_mx(
             out=out_codes[:].bitcast(FP8X4), scales=out_scales[:], in_=rounded[:].rearrange("p v t -> p (v t)")
         )

@@ -73,12 +73,12 @@ def tile_picked_zmodd_none_po_kernel(
         x_table.append(load_words(1))
         load_scales()
         load_weight(1, 0)
-        load_weight(1, 1, 384)
+        load_weight(1, 1)
         cen_t = load_list(cen, "cen_t")
-        load_weight(0, 0, 256)
-        load_weight(0, 1, 384)
+        load_weight(0, 0)
+        load_weight(0, 1)
         pos_t = [load_list(pos1, "pos1_t")]
-        load_weight(2, 0, 256)
+        load_weight(2, 0)
         pos_t.append(load_list(pos2, "pos2_t"))
         load_weight(2, 1)
         pos_t.append(load_list(pos3, "pos3_t"))

@@ -56,20 +56,17 @@ def tile_picked_zmodd_none_po_kernel(
             return table
 
         def load_scales():
-            for q in range(4):
+            for q in (0, 2, 1, 3):
                 nc.sync.dma_start(
                     out=x_planes[32 * q : 32 * q + 4 * PASSES, :].bitcast(I32),
                     in_=x_scales[:, 4 * q : 4 * q + 4, :].bitcast(I32),
                 )
 
-        warm = tile([P, 2], F32, "warm")
-        nc.gpsimd.memset(warm[:, 0:1], 0.0)
-        nc.scalar.activation(warm[:, 1:2], warm[:, 0:1], SIGMOID)
 
         x_planes = tile([P, T], U8, "x_planes")
-        nc.vector.memset(x_planes[:].bitcast(I32), 0)
-        offs_t = load_list(offs, "offs_t")
+        nc.gpsimd.memset(x_planes[:].bitcast(I32), 0)
         x_table = [load_words(0)]
+        offs_t = load_list(offs, "offs_t")
         x_table.append(load_words(1))
         load_scales()
         load_weight(1, 0)
@@ -79,11 +76,11 @@ def tile_picked_zmodd_none_po_kernel(
         load_weight(0, 1)
         pos_t = [load_list(pos1, "pos1_t")]
         load_weight(2, 0)
-        pos_t.append(load_list(pos2, "pos2_t"))
         load_weight(2, 1)
-        pos_t.append(load_list(pos3, "pos3_t"))
         load_weight(3, 0)
         load_weight(3, 1)
+        pos_t.append(load_list(pos2, "pos2_t"))
+        pos_t.append(load_list(pos3, "pos3_t"))
 
         x_codes = [tile([P, S], U32, "x_codes%d" % g) for g in range(PASSES)]
         x_bytes = tile([P, S], U8, "x_bytes")
@@ -144,11 +141,15 @@ def tile_picked_zmodd_none_po_kernel(
         pick_words(0)
         pick_words(1)
         pick_bytes()
-        whole_pass(1, 0, vector, scalar)
-        whole_pass(1, 1, vector, scalar)
+        whole_pass(1, 0)
+        whole_pass(1, 1)
         whole_pass(0, 0)
         whole_pass(0, 1)
-        for t in range(PACK):
+        rows[1, 0] = tile([P, S], F32, "rows1_0")
+        nc.scalar.activation(rows[1, 0][:], banks[1, 0][:], SIGMOID)
+        picked[1, 0] = tile([P, V], F32, "mask1_0")
+        nc.vector.tensor_copy(picked[1, 0][:], rows[1, 0][:].indirect(cen_t[:]))
+        for t in range(1, PACK):
             empty(1, t)
             pick(1, t)
         whole_pass(2, 0)
@@ -176,21 +177,36 @@ def tile_picked_zmodd_none_po_kernel(
         terms2 = tile([P, PACK, V], F32, "terms2")
         result = tile([P, PACK, V], F32, "result")
         out_rows = out_0.rearrange("(p t) v -> p t v", t=PACK)
-        for t in range(PACK):
+        for t in range(PACK - 1):
             empty(3, t)
             pick(3, t)
             term(3, t, terms2[:, t, :])
             nc.vector.tensor_add(result[:, t, :], partial[:, t, :], terms2[:, t, :])
             nc.sync.dma_start(out=out_rows[:, t, :], in_=result[:, t, :])
+        last = PACK - 1
+        empty(3, last)
+        halves = [(slice(a * V // 2, (a + 1) * V // 2), slice(a * V // 32, (a + 1) * V // 32)) for a in range(2)]
+        mask = tile([P, V], F32, "last_mask")
+        for cols, entries in halves:
+            nc.scalar.activation(mask[:, cols], rows[3, last][:].indirect(cen_t[:, entries]), SIGMOID)
+        for cols, entries in halves:
+            nc.vector.tensor_tensor(terms2[:, last, cols], rows[0, last][:].indirect(pos_t[2][:, entries]), mask[:, cols], MULT)
+        for cols, entries in halves:
+            nc.vector.tensor_add(result[:, last, cols], partial[:, last, cols], terms2[:, last, cols])
+        nc.sync.dma_start(out=out_rows[:, last, :], in_=result[:, last, :])
 
         rounded = tile([P, V, PACK], BF16, "rounded")
         scalar(rounded[:, :, 0:2], result[:, 0:2, :].rearrange("p t v -> p v t"))
-        vector(rounded[:, :, 2:4], result[:, 2:4, :].rearrange("p t v -> p v t"))
+        for cols, entries in halves:
+            vector(rounded[:, cols, 2:4], result[:, 2:4, cols].rearrange("p t v -> p v t"))
         out_codes = tile([P, V], U32, "out_codes")
         out_scales = tile([P, V], U8, "out_scales")
-        nc.vector.quantize_mx(
-            out=out_codes[:].bitcast(FP8X4), scales=out_scales[:], in_=rounded[:].rearrange("p v t -> p (v t)")
-        )
+        for cols, entries in halves:
+            nc.vector.quantize_mx(
+                out=out_codes[:, cols].bitcast(FP8X4),
+                scales=out_scales[:, cols],
+                in_=rounded[:, cols, :].rearrange("p v t -> p (v t)"),
+            )
         nc.sync.dma_start(out=out_1[0].rearrange("p c r -> p (c r)").bitcast(I32), in_=out_codes[:].bitcast(I32))
         for q in range(4):
             queue = nc.scalar if q % 2 else nc.sync

@@ -77,10 +77,11 @@ def tile_picked_zmodd_none_po_kernel(
         pos_t = [load_list(pos1, "pos1_t")]
         load_weight(2, 0)
         load_weight(2, 1)
+        third = load_list(pos3, "pos3_t")
         load_weight(3, 0)
         load_weight(3, 1)
         pos_t.append(load_list(pos2, "pos2_t"))
-        pos_t.append(load_list(pos3, "pos3_t"))
+        pos_t.append(third)
 
         x_codes = [tile([P, S], U32, "x_codes%d" % g) for g in range(PASSES)]
         x_bytes = tile([P, S], U8, "x_bytes")
@@ -164,6 +165,8 @@ def tile_picked_zmodd_none_po_kernel(
         term(1, PACK - 1, fourth[:])
         multiply(2, 1, 1)
         whole_pass(3, 0, vector, scalar)
+        fetched = tile([P, V], F32, "fetched", "dealt3_0_0")
+        nc.vector.tensor_copy(fetched[:], rows[0, PACK - 1][:].indirect(pos_t[2][:]))
         whole_pass(3, 1)
         for t in range(PACK):
             empty(2, t)
@@ -190,7 +193,7 @@ def tile_picked_zmodd_none_po_kernel(
         for cols, entries in halves:
             nc.scalar.activation(mask[:, cols], rows[3, last][:].indirect(cen_t[:, entries]), SIGMOID)
         for cols, entries in halves:
-            nc.vector.tensor_tensor(terms2[:, last, cols], rows[0, last][:].indirect(pos_t[2][:, entries]), mask[:, cols], MULT)
+            nc.vector.tensor_mul(terms2[:, last, cols], fetched[:, cols], mask[:, cols])
         for cols, entries in halves:
             nc.vector.tensor_add(result[:, last, cols], partial[:, last, cols], terms2[:, last, cols])
         nc.sync.dma_start(out=out_rows[:, last, :], in_=result[:, last, :])

@@ -74,8 +74,8 @@ def tile_picked_zmodd_none_po_kernel(
         cen_t = load_list(cen, "cen_t")
         load_weight(0, 0)
         load_weight(0, 1)
-        pos_t = [load_list(pos1, "pos1_t")]
         load_weight(2, 0)
+        pos_t = [load_list(pos1, "pos1_t")]
         load_weight(2, 1)
         third = load_list(pos3, "pos3_t")
         load_weight(3, 0)
@@ -101,6 +101,21 @@ def tile_picked_zmodd_none_po_kernel(
                 for h in range(2):
                     src = piece[:].rearrange("p j (m h t) -> p h m j t", h=2, t=2)[:, h]
                     copies[h](dealt[w, g, h][:, :, span].rearrange("p t m j -> p m j t"), src)
+
+        def round_half(w, g, h, copy, tag=None):
+            dealt[w, g, h] = tile([P, 2, P, PACK], BF16, "dealt%d_%d_%d" % (w, g, h), tag)
+            piece, span = raw[w, g][0]
+            src = piece[:].rearrange("p j (m h t) -> p h m j t", h=2, t=2)[:, h]
+            copy(dealt[w, g, h][:].rearrange("p t m j -> p m j t"), src)
+
+        def deal_shared(w, g, split):
+            piece, span = raw[w, g][0]
+            for h in range(2):
+                dealt[w, g, h] = tile([P, 2, P, PACK], BF16, "dealt%d_%d_%d" % (w, g, h))
+                src = piece[:].rearrange("p j (m h t) -> p h m j t", h=2, t=2)[:, h]
+                dst = dealt[w, g, h][:].rearrange("p t m j -> p m j t")
+                vector(dst[:, :split], src[:, :split])
+                scalar(dst[:, split:], src[:, split:])
 
         def multiply(w, g, h, tag=None):
             codes = tile([P, 2 * P], U32, "codes%d_%d_%d" % (w, g, h), tag)
@@ -139,6 +154,9 @@ def tile_picked_zmodd_none_po_kernel(
         def term(w, t, out):
             nc.vector.tensor_tensor(out, rows[0, t][:].indirect(pos_t[w - 1][:]), picked[w, t][:], MULT)
 
+        def fetch(w, t, out):
+            nc.vector.tensor_copy(out, rows[0, t][:].indirect(pos_t[w - 1][:]))
+
         pick_words(0)
         pick_words(1)
         pick_bytes()
@@ -150,9 +168,12 @@ def tile_picked_zmodd_none_po_kernel(
         nc.scalar.activation(rows[1, 0][:], banks[1, 0][:], SIGMOID)
         picked[1, 0] = tile([P, V], F32, "mask1_0")
         nc.vector.tensor_copy(picked[1, 0][:], rows[1, 0][:].indirect(cen_t[:]))
-        for t in range(1, PACK):
-            empty(1, t)
-            pick(1, t)
+        empty(1, 1)
+        empty(1, 2)
+        pick(1, 1)
+        empty(1, 3)
+        pick(1, 2)
+        pick(1, 3)
         whole_pass(2, 0)
         for t in range(PACK):
             empty(0, t)
@@ -161,22 +182,26 @@ def tile_picked_zmodd_none_po_kernel(
         for t in range(PACK - 1):
             term(1, t, early[:, t, :])
         multiply(2, 1, 0)
-        fourth = tile([P, V], F32, "fourth", "dealt2_1_0")
-        term(1, PACK - 1, fourth[:])
+        between = tile([P, 2, V], F32, "between", "dealt2_1_0")
+        fourth, fetched = between[:, 0, :], between[:, 1, :]
+        term(1, PACK - 1, fourth)
+        fetch(3, PACK - 1, fetched)
         multiply(2, 1, 1)
-        whole_pass(3, 0, vector, scalar)
-        fetched = tile([P, V], F32, "fetched", "dealt3_0_0")
-        nc.vector.tensor_copy(fetched[:], rows[0, PACK - 1][:].indirect(pos_t[2][:]))
+        deal_shared(3, 0, 72)
+        multiply(3, 0, 0)
+        multiply(3, 0, 1)
         whole_pass(3, 1)
-        for t in range(PACK):
+        for t in (0, 2):
             empty(2, t)
+            empty(2, t + 1)
             pick(2, t)
+            pick(2, t + 1)
         terms1 = tile([P, PACK, V], F32, "terms1", "dealt3_1_0")
         for t in range(PACK):
             term(2, t, terms1[:, t, :])
         partial = tile([P, PACK, V], F32, "partial")
         nc.vector.tensor_add(partial[:, : PACK - 1, :], early[:], terms1[:, : PACK - 1, :])
-        nc.vector.tensor_add(partial[:, PACK - 1, :], fourth[:], terms1[:, PACK - 1, :])
+        nc.vector.tensor_add(partial[:, PACK - 1, :], fourth, terms1[:, PACK - 1, :])
         terms2 = tile([P, PACK, V], F32, "terms2")
         result = tile([P, PACK, V], F32, "result")
         out_rows = out_0.rearrange("(p t) v -> p t v", t=PACK)

@@ -187,7 +187,7 @@ def tile_picked_zmodd_none_po_kernel(
         term(1, PACK - 1, fourth)
         fetch(3, PACK - 1, fetched)
         multiply(2, 1, 1)
-        deal_shared(3, 0, 72)
+        deal_shared(3, 0, 96)
         multiply(3, 0, 0)
         multiply(3, 0, 1)
         whole_pass(3, 1)

@@ -19,6 +19,10 @@ P = 128
 PACK = 4
 K_PASS = P * PACK
 PASSES = K // K_PASS
+QUADRANT = 32
+LIST_GROUP = 16
+LAST = PACK - 1
+VECTOR_SHARE = 84
 
 
 def tile_picked_zmodd_none_po_kernel(
@@ -26,10 +30,10 @@ def tile_picked_zmodd_none_po_kernel(
 ):
     nc = tc.nc
     weights = (w0, w1, w2, w3)
-    vector, scalar = nc.vector.tensor_copy, nc.scalar.copy
+    on_vector, on_scalar = nc.vector.tensor_copy, nc.scalar.copy
     with ExitStack() as ctx:
         keep = ctx.enter_context(tc.tile_pool(name="keep", bufs=1))
-        psum = ctx.enter_context(tc.psum_pool(name="psum", bufs=8))
+        psum = ctx.enter_context(tc.psum_pool(name="psum", bufs=2 * PACK))
 
         def tile(shape, dtype, name, tag=None):
             return keep.tile(shape, dtype, name=name, tag=tag or name, align_bytes=64)
@@ -41,157 +45,139 @@ def tile_picked_zmodd_none_po_kernel(
 
         raw = {}
 
-        def load_weight(w, g, *cuts):
-            edges = (0,) + cuts + (N,)
-            raw[w, g] = []
-            for first, last in zip(edges, edges[1:]):
-                piece = tile([P, PACK, last - first], F32, "raw%d_%d_%d" % (w, g, first))
-                rows = weights[w][g * K_PASS : (g + 1) * K_PASS, first:last]
-                nc.sync.dma_start(out=piece[:], in_=rows.rearrange("(p j) c -> p j c", j=PACK))
-                raw[w, g].append((piece, slice(first // PACK, last // PACK)))
+        def load_weight(w, g):
+            raw[w, g] = tile([P, PACK, N], F32, "raw%d_%d" % (w, g))
+            k_rows = weights[w][g * K_PASS : (g + 1) * K_PASS, :]
+            nc.sync.dma_start(out=raw[w, g][:], in_=k_rows.rearrange("(p j) c -> p j c", j=PACK))
 
         def load_words(g):
             table = tile([P, T], I32, "x_table%d" % g)
             nc.sync.dma_start(out=table[:], in_=x_words[g].rearrange("p c r -> p (c r)").bitcast(I32))
             return table
 
-        def load_scales():
-            for q in (0, 2, 1, 3):
-                nc.sync.dma_start(
-                    out=x_planes[32 * q : 32 * q + 4 * PASSES, :].bitcast(I32),
-                    in_=x_scales[:, 4 * q : 4 * q + 4, :].bitcast(I32),
-                )
-
-
         x_planes = tile([P, T], U8, "x_planes")
         nc.gpsimd.memset(x_planes[:].bitcast(I32), 0)
         x_table = [load_words(0)]
         offs_t = load_list(offs, "offs_t")
         x_table.append(load_words(1))
-        load_scales()
+        for q in (0, 2, 1, 3):
+            nc.sync.dma_start(
+                out=x_planes[QUADRANT * q : QUADRANT * q + PACK * PASSES, :].bitcast(I32),
+                in_=x_scales[:, PACK * q : PACK * (q + 1), :].bitcast(I32),
+            )
         load_weight(1, 0)
         load_weight(1, 1)
         cen_t = load_list(cen, "cen_t")
         load_weight(0, 0)
         load_weight(0, 1)
         load_weight(2, 0)
-        pos_t = [load_list(pos1, "pos1_t")]
+        pos1_t = load_list(pos1, "pos1_t")
         load_weight(2, 1)
-        third = load_list(pos3, "pos3_t")
+        pos3_t = load_list(pos3, "pos3_t")
         load_weight(3, 0)
         load_weight(3, 1)
-        pos_t.append(load_list(pos2, "pos2_t"))
-        pos_t.append(third)
+        pos2_t = load_list(pos2, "pos2_t")
+        pos_t = {1: pos1_t, 2: pos2_t, 3: pos3_t}
 
         x_codes = [tile([P, S], U32, "x_codes%d" % g) for g in range(PASSES)]
         x_bytes = tile([P, S], U8, "x_bytes")
 
-        def pick_words(g):
-            nc.vector.tensor_copy(x_codes[g][:], x_table[g][:].bitcast(U32).indirect(offs_t[:]))
+        dealt, banks, rows, picked = {}, {}, {}, {}
 
-        def pick_bytes():
-            nc.vector.tensor_copy(x_bytes[:], x_planes[:].indirect(offs_t[:]))
+        def deal_views(w, g, h):
+            src = raw[w, g][:].rearrange("p j (m h u) -> p h m j u", h=2, u=2)[:, h]
+            return dealt[w, g, h][:].rearrange("p u m j -> p m j u"), src
 
-        dealt, banks, rows, picked, terms = {}, {}, {}, {}, {}
+        def dealt_tile(w, g, h):
+            dealt[w, g, h] = tile([P, 2, P, PACK], BF16, "dealt%d_%d_%d" % (w, g, h))
 
-        def deal(w, g, copies):
+        def deal(w, g, copy):
             for h in range(2):
-                dealt[w, g, h] = tile([P, 2, P, PACK], BF16, "dealt%d_%d_%d" % (w, g, h))
-            for piece, span in raw[w, g]:
-                for h in range(2):
-                    src = piece[:].rearrange("p j (m h t) -> p h m j t", h=2, t=2)[:, h]
-                    copies[h](dealt[w, g, h][:, :, span].rearrange("p t m j -> p m j t"), src)
-
-        def round_half(w, g, h, copy, tag=None):
-            dealt[w, g, h] = tile([P, 2, P, PACK], BF16, "dealt%d_%d_%d" % (w, g, h), tag)
-            piece, span = raw[w, g][0]
-            src = piece[:].rearrange("p j (m h t) -> p h m j t", h=2, t=2)[:, h]
-            copy(dealt[w, g, h][:].rearrange("p t m j -> p m j t"), src)
-
-        def deal_shared(w, g, split):
-            piece, span = raw[w, g][0]
+                dealt_tile(w, g, h)
             for h in range(2):
-                dealt[w, g, h] = tile([P, 2, P, PACK], BF16, "dealt%d_%d_%d" % (w, g, h))
-                src = piece[:].rearrange("p j (m h t) -> p h m j t", h=2, t=2)[:, h]
-                dst = dealt[w, g, h][:].rearrange("p t m j -> p m j t")
-                vector(dst[:, :split], src[:, :split])
-                scalar(dst[:, split:], src[:, split:])
+                copy(*deal_views(w, g, h))
 
-        def multiply(w, g, h, tag=None):
-            codes = tile([P, 2 * P], U32, "codes%d_%d_%d" % (w, g, h), tag)
+        def deal_shared(w, g):
+            for h in range(2):
+                dealt_tile(w, g, h)
+                dst, src = deal_views(w, g, h)
+                on_vector(dst[:, :VECTOR_SHARE], src[:, :VECTOR_SHARE])
+                on_scalar(dst[:, VECTOR_SHARE:], src[:, VECTOR_SHARE:])
+
+        def multiply(w, g, h):
+            codes = tile([P, 2 * P], U32, "codes%d_%d_%d" % (w, g, h))
             scales = tile([P, 2 * P], U8, "scales%d_%d_%d" % (w, g, h))
             nc.vector.quantize_mx(
-                out=codes[:].bitcast(FP8X4), scales=scales[:], in_=dealt[w, g, h][:].rearrange("p t m j -> p (t m j)")
+                out=codes[:].bitcast(FP8X4), scales=scales[:], in_=dealt[w, g, h][:].rearrange("p u m j -> p (u m j)")
             )
-            for s in range(2):
-                t = 2 * h + s
+            for u in range(2):
+                t = 2 * h + u
                 if g == 0:
                     banks[w, t] = psum.tile([P, S], F32, name="bank")
-                cols = slice(s * P, (s + 1) * P)
+                cols = slice(u * P, (u + 1) * P)
                 nc.tensor.matmul_mx(
                     out=banks[w, t][:],
                     lhsT=codes[:, cols].bitcast(FP8X4),
                     lhsT_scale=scales[:, cols],
                     rhs=x_codes[g][:].bitcast(FP8X4),
-                    rhs_scale=x_bytes[4 * g :, :],
+                    rhs_scale=x_bytes[PACK * g :, :],
                     start=(g == 0),
                     stop=(g == PASSES - 1),
                 )
 
-        def whole_pass(w, g, first=vector, second=vector):
-            deal(w, g, (first, second))
+        def vector_pass(w, g):
+            deal(w, g, on_vector)
             multiply(w, g, 0)
             multiply(w, g, 1)
 
-        def empty(w, t, copy=scalar, tag=None):
-            rows[w, t] = tile([P, S], F32, "rows%d_%d" % (w, t), tag)
-            copy(rows[w, t][:], banks[w, t][:])
+        def empty(w, t):
+            rows[w, t] = tile([P, S], F32, "rows%d_%d" % (w, t))
+            on_scalar(rows[w, t][:], banks[w, t][:])
 
-        def pick(w, t, tag=None):
-            picked[w, t] = tile([P, V], F32, "mask%d_%d" % (w, t), tag)
+        def pick(w, t):
+            picked[w, t] = tile([P, V], F32, "mask%d_%d" % (w, t))
             nc.scalar.activation(picked[w, t][:], rows[w, t][:].indirect(cen_t[:]), SIGMOID)
 
         def term(w, t, out):
-            nc.vector.tensor_tensor(out, rows[0, t][:].indirect(pos_t[w - 1][:]), picked[w, t][:], MULT)
+            nc.vector.tensor_tensor(out, rows[0, t][:].indirect(pos_t[w][:]), picked[w, t][:], MULT)
 
-        def fetch(w, t, out):
-            nc.vector.tensor_copy(out, rows[0, t][:].indirect(pos_t[w - 1][:]))
+        for g in range(PASSES):
+            on_vector(x_codes[g][:], x_table[g][:].bitcast(U32).indirect(offs_t[:]))
+        on_vector(x_bytes[:], x_planes[:].indirect(offs_t[:]))
 
-        pick_words(0)
-        pick_words(1)
-        pick_bytes()
-        whole_pass(1, 0)
-        whole_pass(1, 1)
-        whole_pass(0, 0)
-        whole_pass(0, 1)
+        for w in (1, 0):
+            for g in range(PASSES):
+                vector_pass(w, g)
         rows[1, 0] = tile([P, S], F32, "rows1_0")
         nc.scalar.activation(rows[1, 0][:], banks[1, 0][:], SIGMOID)
         picked[1, 0] = tile([P, V], F32, "mask1_0")
-        nc.vector.tensor_copy(picked[1, 0][:], rows[1, 0][:].indirect(cen_t[:]))
+        on_vector(picked[1, 0][:], rows[1, 0][:].indirect(cen_t[:]))
         empty(1, 1)
         empty(1, 2)
         pick(1, 1)
         empty(1, 3)
         pick(1, 2)
         pick(1, 3)
-        whole_pass(2, 0)
+
+        vector_pass(2, 0)
         for t in range(PACK):
             empty(0, t)
-        deal(2, 1, (scalar, scalar))
-        early = tile([P, PACK - 1, V], F32, "early", "dealt2_0_0")
-        for t in range(PACK - 1):
+        deal(2, 1, on_scalar)
+        early = tile([P, LAST, V], F32, "early", "dealt2_0_0")
+        for t in range(LAST):
             term(1, t, early[:, t, :])
         multiply(2, 1, 0)
         between = tile([P, 2, V], F32, "between", "dealt2_1_0")
         fourth, fetched = between[:, 0, :], between[:, 1, :]
-        term(1, PACK - 1, fourth)
-        fetch(3, PACK - 1, fetched)
+        term(1, LAST, fourth)
+        on_vector(fetched, rows[0, LAST][:].indirect(pos_t[3][:]))
         multiply(2, 1, 1)
-        deal_shared(3, 0, 96)
+
+        deal_shared(3, 0)
         multiply(3, 0, 0)
         multiply(3, 0, 1)
-        whole_pass(3, 1)
-        for t in (0, 2):
+        vector_pass(3, 1)
+        for t in range(0, PACK, 2):
             empty(2, t)
             empty(2, t + 1)
             pick(2, t)
@@ -200,44 +186,47 @@ def tile_picked_zmodd_none_po_kernel(
         for t in range(PACK):
             term(2, t, terms1[:, t, :])
         partial = tile([P, PACK, V], F32, "partial")
-        nc.vector.tensor_add(partial[:, : PACK - 1, :], early[:], terms1[:, : PACK - 1, :])
-        nc.vector.tensor_add(partial[:, PACK - 1, :], fourth, terms1[:, PACK - 1, :])
+        nc.vector.tensor_add(partial[:, :LAST, :], early[:], terms1[:, :LAST, :])
+        nc.vector.tensor_add(partial[:, LAST, :], fourth, terms1[:, LAST, :])
+
         terms2 = tile([P, PACK, V], F32, "terms2")
         result = tile([P, PACK, V], F32, "result")
         out_rows = out_0.rearrange("(p t) v -> p t v", t=PACK)
-        for t in range(PACK - 1):
+        for t in range(LAST):
             empty(3, t)
             pick(3, t)
             term(3, t, terms2[:, t, :])
             nc.vector.tensor_add(result[:, t, :], partial[:, t, :], terms2[:, t, :])
             nc.sync.dma_start(out=out_rows[:, t, :], in_=result[:, t, :])
-        last = PACK - 1
-        empty(3, last)
-        halves = [(slice(a * V // 2, (a + 1) * V // 2), slice(a * V // 32, (a + 1) * V // 32)) for a in range(2)]
-        mask = tile([P, V], F32, "last_mask")
-        for cols, entries in halves:
-            nc.scalar.activation(mask[:, cols], rows[3, last][:].indirect(cen_t[:, entries]), SIGMOID)
-        for cols, entries in halves:
-            nc.vector.tensor_mul(terms2[:, last, cols], fetched[:, cols], mask[:, cols])
-        for cols, entries in halves:
-            nc.vector.tensor_add(result[:, last, cols], partial[:, last, cols], terms2[:, last, cols])
-        nc.sync.dma_start(out=out_rows[:, last, :], in_=result[:, last, :])
+        empty(3, LAST)
+        half, half_list = V // 2, V // 2 // LIST_GROUP
+        halves = [slice(a * half, (a + 1) * half) for a in range(2)]
+        last_mask = tile([P, V], F32, "last_mask")
+        for a, cols in enumerate(halves):
+            entries = cen_t[:, a * half_list : (a + 1) * half_list]
+            nc.scalar.activation(last_mask[:, cols], rows[3, LAST][:].indirect(entries), SIGMOID)
+        for cols in halves:
+            nc.vector.tensor_mul(terms2[:, LAST, cols], fetched[:, cols], last_mask[:, cols])
+        for cols in halves:
+            nc.vector.tensor_add(result[:, LAST, cols], partial[:, LAST, cols], terms2[:, LAST, cols])
+        nc.sync.dma_start(out=out_rows[:, LAST, :], in_=result[:, LAST, :])
 
         rounded = tile([P, V, PACK], BF16, "rounded")
-        scalar(rounded[:, :, 0:2], result[:, 0:2, :].rearrange("p t v -> p v t"))
-        for cols, entries in halves:
-            vector(rounded[:, cols, 2:4], result[:, 2:4, cols].rearrange("p t v -> p v t"))
+        on_scalar(rounded[:, :, 0:2], result[:, 0:2, :].rearrange("p t v -> p v t"))
+        for cols in halves:
+            on_vector(rounded[:, cols, 2:4], result[:, 2:4, cols].rearrange("p t v -> p v t"))
         out_codes = tile([P, V], U32, "out_codes")
         out_scales = tile([P, V], U8, "out_scales")
-        for cols, entries in halves:
+        for cols in halves:
             nc.vector.quantize_mx(
                 out=out_codes[:, cols].bitcast(FP8X4),
                 scales=out_scales[:, cols],
                 in_=rounded[:, cols, :].rearrange("p v t -> p (v t)"),
             )
         nc.sync.dma_start(out=out_1[0].rearrange("p c r -> p (c r)").bitcast(I32), in_=out_codes[:].bitcast(I32))
-        for q in range(4):
+        for q in range(P // QUADRANT):
             queue = nc.scalar if q % 2 else nc.sync
             queue.dma_start(
-                out=out_2[0, 4 * q : 4 * q + 4, :].bitcast(I32), in_=out_scales[32 * q : 32 * q + 4, :].bitcast(I32)
+                out=out_2[0, PACK * q : PACK * (q + 1), :].bitcast(I32),
+                in_=out_scales[QUADRANT * q : QUADRANT * q + PACK, :].bitcast(I32),
             )

@@ -22,7 +22,7 @@ PASSES = K // K_PASS
 QUADRANT = 32
 LIST_GROUP = 16
 LAST = PACK - 1
-VECTOR_SHARE = 84
+VECTOR_SHARE = 100
 
 
 def tile_picked_zmodd_none_po_kernel(
@@ -189,16 +189,23 @@ def tile_picked_zmodd_none_po_kernel(
         nc.vector.tensor_add(partial[:, :LAST, :], early[:], terms1[:, :LAST, :])
         nc.vector.tensor_add(partial[:, LAST, :], fourth, terms1[:, LAST, :])
 
-        terms2 = tile([P, PACK, V], F32, "terms2")
         result = tile([P, PACK, V], F32, "result")
         out_rows = out_0.rearrange("(p t) v -> p t v", t=PACK)
-        for t in range(LAST):
+        for t in range(2):
             empty(3, t)
+        for t in range(2):
             pick(3, t)
-            term(3, t, terms2[:, t, :])
-            nc.vector.tensor_add(result[:, t, :], partial[:, t, :], terms2[:, t, :])
-            nc.sync.dma_start(out=out_rows[:, t, :], in_=result[:, t, :])
-        empty(3, LAST)
+        first = tile([P, 2, V], F32, "first", "rows3_1")
+        for t in range(2):
+            term(3, t, first[:, t, :])
+        for t in range(2):
+            nc.vector.tensor_add(result[:, t, :], partial[:, t, :], first[:, t, :])
+        nc.sync.dma_start(out=out_rows[:, :2, :], in_=result[:, :2, :])
+        for t in range(2, PACK):
+            empty(3, t)
+        pick(3, 2)
+        second = tile([P, 2, V], F32, "second")
+        term(3, 2, second[:, 0, :])
         half, half_list = V // 2, V // 2 // LIST_GROUP
         halves = [slice(a * half, (a + 1) * half) for a in range(2)]
         last_mask = tile([P, V], F32, "last_mask")
@@ -206,10 +213,10 @@ def tile_picked_zmodd_none_po_kernel(
             entries = cen_t[:, a * half_list : (a + 1) * half_list]
             nc.scalar.activation(last_mask[:, cols], rows[3, LAST][:].indirect(entries), SIGMOID)
         for cols in halves:
-            nc.vector.tensor_mul(terms2[:, LAST, cols], fetched[:, cols], last_mask[:, cols])
+            nc.vector.tensor_mul(second[:, 1, cols], fetched[:, cols], last_mask[:, cols])
         for cols in halves:
-            nc.vector.tensor_add(result[:, LAST, cols], partial[:, LAST, cols], terms2[:, LAST, cols])
-        nc.sync.dma_start(out=out_rows[:, LAST, :], in_=result[:, LAST, :])
+            nc.vector.tensor_add(result[:, 2:, cols], partial[:, 2:, cols], second[:, :, cols])
+        nc.sync.dma_start(out=out_rows[:, 2:, :], in_=result[:, 2:, :])
 
         rounded = tile([P, V, PACK], BF16, "rounded")
         on_scalar(rounded[:, :, 0:2], result[:, 0:2, :].rearrange("p t v -> p v t"))

@@ -1,6 +1,7 @@
 from contextlib import ExitStack
 
 import concourse.mybir as mybir
+from concourse.masks import make_identity
 
 K, T, S, V, N = 1024, 1024, 512, 256, 512
 FLOPS = 4 * 2 * K * N * S
@@ -79,6 +80,9 @@ def tile_picked_zmodd_none_po_kernel(
         pos2_t = load_list(pos2, "pos2_t")
         pos_t = {1: pos1_t, 2: pos2_t, 3: pos3_t}
 
+        identity = tile([P, P], F32, "identity")
+        make_identity(nc, identity[:])
+
         x_codes = [tile([P, S], U32, "x_codes%d" % g) for g in range(PASSES)]
         x_bytes = tile([P, S], U8, "x_bytes")
 
@@ -130,8 +134,8 @@ def tile_picked_zmodd_none_po_kernel(
             multiply(w, g, 0)
             multiply(w, g, 1)
 
-        def empty(w, t):
-            rows[w, t] = tile([P, S], F32, "rows%d_%d" % (w, t))
+        def empty(w, t, tag=None):
+            rows[w, t] = tile([P, S], F32, "rows%d_%d" % (w, t), tag)
             on_scalar(rows[w, t][:], banks[w, t][:])
 
         def pick(w, t):
@@ -163,9 +167,11 @@ def tile_picked_zmodd_none_po_kernel(
         for t in range(PACK):
             empty(0, t)
         deal(2, 1, on_scalar)
-        early = tile([P, LAST, V], F32, "early", "dealt2_0_0")
-        for t in range(LAST):
+        early = tile([P, 2, V], F32, "early", "dealt2_0_0")
+        for t in range(2):
             term(1, t, early[:, t, :])
+        third = tile([P, V], F32, "third", "dealt2_0_1")
+        term(1, 2, third[:])
         multiply(2, 1, 0)
         between = tile([P, 2, V], F32, "between", "dealt2_1_0")
         fourth, fetched = between[:, 0, :], between[:, 1, :]
@@ -173,21 +179,18 @@ def tile_picked_zmodd_none_po_kernel(
         on_vector(fetched, rows[0, LAST][:].indirect(pos_t[3][:]))
         multiply(2, 1, 1)
 
-        deal_shared(3, 0)
-        multiply(3, 0, 0)
-        multiply(3, 0, 1)
+        vector_pass(3, 0)
         vector_pass(3, 1)
         for t in range(0, PACK, 2):
             empty(2, t)
             empty(2, t + 1)
             pick(2, t)
             pick(2, t + 1)
-        terms1 = tile([P, PACK, V], F32, "terms1", "dealt3_1_0")
+        terms1 = [tile([P, 2, V], F32, "terms1_%d" % h, "dealt3_1_%d" % h) for h in range(2)]
         for t in range(PACK):
-            term(2, t, terms1[:, t, :])
-        partial = tile([P, PACK, V], F32, "partial")
-        nc.vector.tensor_add(partial[:, :LAST, :], early[:], terms1[:, :LAST, :])
-        nc.vector.tensor_add(partial[:, LAST, :], fourth, terms1[:, LAST, :])
+            term(2, t, terms1[t // 2][:, t % 2, :])
+        partial = tile([P, 2, V], F32, "partial")
+        nc.vector.tensor_add(partial[:], early[:], terms1[0][:])
 
         result = tile([P, PACK, V], F32, "result")
         out_rows = out_0.rearrange("(p t) v -> p t v", t=PACK)
@@ -204,18 +207,29 @@ def tile_picked_zmodd_none_po_kernel(
         for t in range(2, PACK):
             empty(3, t)
         pick(3, 2)
+        turned = psum.tile([P, 2, V], F32, name="bank")
+        blocks = [(u, slice(a * P, (a + 1) * P)) for u in range(2) for a in range(V // P)]
+        for u, cols in blocks:
+            for n, part in enumerate(((third[:], fourth)[u], terms1[1][:, u, :])):
+                nc.tensor.matmul(turned[:, u, cols], part[:, cols], identity[:], start=(n == 0), stop=(n == 1), is_transpose=True)
+        staged = tile([P, 2, V], F32, "staged")
+        on_scalar(staged[:], turned[:])
+        back = [psum.tile([P, 2, P], F32, name="bank") for a in range(V // P)]
+        for a in range(V // P):
+            for u in range(2):
+                nc.tensor.transpose(back[a][:, u, :], staged[:, u, a * P : (a + 1) * P], identity[:])
         second = tile([P, 2, V], F32, "second")
         term(3, 2, second[:, 0, :])
         half, half_list = V // 2, V // 2 // LIST_GROUP
         halves = [slice(a * half, (a + 1) * half) for a in range(2)]
-        last_mask = tile([P, V], F32, "last_mask")
+        last_mask = tile([P, V], F32, "last_mask", "dealt3_1_1")
         for a, cols in enumerate(halves):
             entries = cen_t[:, a * half_list : (a + 1) * half_list]
             nc.scalar.activation(last_mask[:, cols], rows[3, LAST][:].indirect(entries), SIGMOID)
         for cols in halves:
             nc.vector.tensor_mul(second[:, 1, cols], fetched[:, cols], last_mask[:, cols])
-        for cols in halves:
-            nc.vector.tensor_add(result[:, 2:, cols], partial[:, 2:, cols], second[:, :, cols])
+        for a, cols in enumerate(halves):
+            nc.vector.tensor_add(result[:, 2:, cols], back[a][:], second[:, :, cols])
         nc.sync.dma_start(out=out_rows[:, 2:, :], in_=result[:, 2:, :])
 
         rounded = tile([P, V, PACK], BF16, "rounded")

@@ -23,7 +23,7 @@ PASSES = K // K_PASS
 QUADRANT = 32
 LIST_GROUP = 16
 LAST = PACK - 1
-VECTOR_SHARE = 100
+VECTOR_SHARE = 116
 
 
 def tile_picked_zmodd_none_po_kernel(
@@ -57,7 +57,7 @@ def tile_picked_zmodd_none_po_kernel(
             return table
 
         x_planes = tile([P, T], U8, "x_planes")
-        nc.gpsimd.memset(x_planes[:].bitcast(I32), 0)
+        nc.vector.memset(x_planes[:].bitcast(I32), 0)
         x_table = [load_words(0)]
         offs_t = load_list(offs, "offs_t")
         x_table.append(load_words(1))
@@ -108,12 +108,17 @@ def tile_picked_zmodd_none_po_kernel(
                 on_vector(dst[:, :VECTOR_SHARE], src[:, :VECTOR_SHARE])
                 on_scalar(dst[:, VECTOR_SHARE:], src[:, VECTOR_SHARE:])
 
-        def multiply(w, g, h):
+        def multiply(w, g, h, by_tile=False):
             codes = tile([P, 2 * P], U32, "codes%d_%d_%d" % (w, g, h))
             scales = tile([P, 2 * P], U8, "scales%d_%d_%d" % (w, g, h))
-            nc.vector.quantize_mx(
-                out=codes[:].bitcast(FP8X4), scales=scales[:], in_=dealt[w, g, h][:].rearrange("p u m j -> p (u m j)")
-            )
+            flat = dealt[w, g, h][:].rearrange("p u m j -> p (u m j)")
+            width = P if by_tile else 2 * P
+            for c in range(0, 2 * P, width):
+                nc.vector.quantize_mx(
+                    out=codes[:, c : c + width].bitcast(FP8X4),
+                    scales=scales[:, c : c + width],
+                    in_=flat[:, PACK * c : PACK * (c + width)],
+                )
             for u in range(2):
                 t = 2 * h + u
                 if g == 0:
@@ -172,14 +177,16 @@ def tile_picked_zmodd_none_po_kernel(
             term(1, t, early[:, t, :])
         third = tile([P, V], F32, "third", "dealt2_0_1")
         term(1, 2, third[:])
-        multiply(2, 1, 0)
-        between = tile([P, 2, V], F32, "between", "dealt2_1_0")
-        fourth, fetched = between[:, 0, :], between[:, 1, :]
+        multiply(2, 1, 0, by_tile=True)
+        between = dealt[2, 1, 0][:].rearrange("p u m j -> p (u m j)").bitcast(F32)
+        fourth, fetched = between[:, :V], between[:, V:]
         term(1, LAST, fourth)
         on_vector(fetched, rows[0, LAST][:].indirect(pos_t[3][:]))
         multiply(2, 1, 1)
 
-        vector_pass(3, 0)
+        deal_shared(3, 0)
+        multiply(3, 0, 0)
+        multiply(3, 0, 1)
         vector_pass(3, 1)
         for t in range(0, PACK, 2):
             empty(2, t)

@@ -23,6 +23,7 @@ PASSES = K // K_PASS
 QUADRANT = 32
 LIST_GROUP = 16
 LAST = PACK - 1
+PIECES = 4
 VECTOR_SHARE = 116
 
 
@@ -139,8 +140,8 @@ def tile_picked_zmodd_none_po_kernel(
             multiply(w, g, 0)
             multiply(w, g, 1)
 
-        def empty(w, t, tag=None):
-            rows[w, t] = tile([P, S], F32, "rows%d_%d" % (w, t), tag)
+        def empty(w, t):
+            rows[w, t] = tile([P, S], F32, "rows%d_%d" % (w, t))
             on_scalar(rows[w, t][:], banks[w, t][:])
 
         def pick(w, t):
@@ -211,6 +212,7 @@ def tile_picked_zmodd_none_po_kernel(
         for t in range(2):
             nc.vector.tensor_add(result[:, t, :], partial[:, t, :], first[:, t, :])
         nc.sync.dma_start(out=out_rows[:, :2, :], in_=result[:, :2, :])
+
         for t in range(2, PACK):
             empty(3, t)
         pick(3, 2)
@@ -218,7 +220,9 @@ def tile_picked_zmodd_none_po_kernel(
         blocks = [(u, slice(a * P, (a + 1) * P)) for u in range(2) for a in range(V // P)]
         for u, cols in blocks:
             for n, part in enumerate(((third[:], fourth)[u], terms1[1][:, u, :])):
-                nc.tensor.matmul(turned[:, u, cols], part[:, cols], identity[:], start=(n == 0), stop=(n == 1), is_transpose=True)
+                nc.tensor.matmul(
+                    turned[:, u, cols], part[:, cols], identity[:], start=(n == 0), stop=(n == 1), is_transpose=True
+                )
         staged = tile([P, 2, V], F32, "staged")
         on_scalar(staged[:], turned[:])
         back = [psum.tile([P, 2, P], F32, name="bank") for a in range(V // P)]
@@ -227,25 +231,28 @@ def tile_picked_zmodd_none_po_kernel(
                 nc.tensor.transpose(back[a][:, u, :], staged[:, u, a * P : (a + 1) * P], identity[:])
         second = tile([P, 2, V], F32, "second")
         term(3, 2, second[:, 0, :])
-        half, half_list = V // 2, V // 2 // LIST_GROUP
-        halves = [slice(a * half, (a + 1) * half) for a in range(2)]
+        pieces = [slice(a * V // PIECES, (a + 1) * V // PIECES) for a in range(PIECES)]
         last_mask = tile([P, V], F32, "last_mask", "dealt3_1_1")
-        for a, cols in enumerate(halves):
-            entries = cen_t[:, a * half_list : (a + 1) * half_list]
+        for cols in pieces:
+            entries = cen_t[:, cols.start // LIST_GROUP : cols.stop // LIST_GROUP]
             nc.scalar.activation(last_mask[:, cols], rows[3, LAST][:].indirect(entries), SIGMOID)
-        for cols in halves:
+        for cols in pieces:
             nc.vector.tensor_mul(second[:, 1, cols], fetched[:, cols], last_mask[:, cols])
-        for a, cols in enumerate(halves):
-            nc.vector.tensor_add(result[:, 2:, cols], back[a][:], second[:, :, cols])
+        for cols in pieces:
+            a, begin = divmod(cols.start, P)
+            nc.vector.tensor_add(result[:, 2:, cols], back[a][:, :, begin : begin + V // PIECES], second[:, :, cols])
         nc.sync.dma_start(out=out_rows[:, 2:, :], in_=result[:, 2:, :])
 
         rounded = tile([P, V, PACK], BF16, "rounded")
-        on_scalar(rounded[:, :, 0:2], result[:, 0:2, :].rearrange("p t v -> p v t"))
-        for cols in halves:
-            on_vector(rounded[:, cols, 2:4], result[:, 2:4, cols].rearrange("p t v -> p v t"))
+        for n, cols in enumerate(pieces):
+            copy = on_scalar if n == 0 else on_vector
+            copy(
+                rounded[:, cols, :].rearrange("p (c i) t -> p c t i", i=PACK),
+                result[:, :, cols].rearrange("p t (c i) -> p c t i", i=PACK),
+            )
         out_codes = tile([P, V], U32, "out_codes")
         out_scales = tile([P, V], U8, "out_scales")
-        for cols in halves:
+        for cols in pieces:
             nc.vector.quantize_mx(
                 out=out_codes[:, cols].bitcast(FP8X4),
                 scales=out_scales[:, cols],

@@ -14,6 +14,7 @@ U16 = mybir.dt.uint16
 U8 = mybir.dt.uint8
 FP8X4 = mybir.dt.float8_e4m3fn_x4
 SIGMOID = mybir.ActivationFunctionType.Sigmoid
+COPY = mybir.ActivationFunctionType.Copy
 MULT = mybir.AluOpType.mult
 
 P = 128
@@ -22,9 +23,9 @@ K_PASS = P * PACK
 PASSES = K // K_PASS
 QUADRANT = 32
 LIST_GROUP = 16
-LAST = PACK - 1
 PIECES = 4
-VECTOR_SHARE = 116
+FUSED1 = 2
+VECTOR_SHARE = 88
 
 
 def tile_picked_zmodd_none_po_kernel(
@@ -67,27 +68,29 @@ def tile_picked_zmodd_none_po_kernel(
                 out=x_planes[QUADRANT * q : QUADRANT * q + PACK * PASSES, :].bitcast(I32),
                 in_=x_scales[:, PACK * q : PACK * (q + 1), :].bitcast(I32),
             )
-        load_weight(1, 0)
-        load_weight(1, 1)
-        cen_t = load_list(cen, "cen_t")
         load_weight(0, 0)
         load_weight(0, 1)
-        load_weight(2, 0)
         pos1_t = load_list(pos1, "pos1_t")
+        load_weight(1, 0)
+        pos2_t = load_list(pos2, "pos2_t")
+        load_weight(1, 1)
+        cen_t = load_list(cen, "cen_t")
+        load_weight(2, 0)
         load_weight(2, 1)
         pos3_t = load_list(pos3, "pos3_t")
         load_weight(3, 0)
         load_weight(3, 1)
-        pos2_t = load_list(pos2, "pos2_t")
         pos_t = {1: pos1_t, 2: pos2_t, 3: pos3_t}
 
         identity = tile([P, P], F32, "identity")
         make_identity(nc, identity[:])
+        warm = tile([P, 1], F32, "warm")
+        nc.scalar.activation(warm[:], identity[:, 0:1], SIGMOID)
 
         x_codes = [tile([P, S], U32, "x_codes%d" % g) for g in range(PASSES)]
         x_bytes = tile([P, S], U8, "x_bytes")
 
-        dealt, banks, rows, picked = {}, {}, {}, {}
+        dealt, banks, rows = {}, {}, {}
 
         def deal_views(w, g, h):
             src = raw[w, g][:].rearrange("p j (m h u) -> p h m j u", h=2, u=2)[:, h]
@@ -96,30 +99,14 @@ def tile_picked_zmodd_none_po_kernel(
         def dealt_tile(w, g, h):
             dealt[w, g, h] = tile([P, 2, P, PACK], BF16, "dealt%d_%d_%d" % (w, g, h))
 
-        def deal(w, g, copy):
-            for h in range(2):
-                dealt_tile(w, g, h)
-            for h in range(2):
-                copy(*deal_views(w, g, h))
-
-        def deal_shared(w, g):
-            for h in range(2):
-                dealt_tile(w, g, h)
-                dst, src = deal_views(w, g, h)
-                on_vector(dst[:, :VECTOR_SHARE], src[:, :VECTOR_SHARE])
-                on_scalar(dst[:, VECTOR_SHARE:], src[:, VECTOR_SHARE:])
-
-        def multiply(w, g, h, by_tile=False):
+        def multiply(w, g, h):
             codes = tile([P, 2 * P], U32, "codes%d_%d_%d" % (w, g, h))
             scales = tile([P, 2 * P], U8, "scales%d_%d_%d" % (w, g, h))
-            flat = dealt[w, g, h][:].rearrange("p u m j -> p (u m j)")
-            width = P if by_tile else 2 * P
-            for c in range(0, 2 * P, width):
-                nc.vector.quantize_mx(
-                    out=codes[:, c : c + width].bitcast(FP8X4),
-                    scales=scales[:, c : c + width],
-                    in_=flat[:, PACK * c : PACK * (c + width)],
-                )
+            nc.vector.quantize_mx(
+                out=codes[:].bitcast(FP8X4),
+                scales=scales[:],
+                in_=dealt[w, g, h][:].rearrange("p u m j -> p (u m j)"),
+            )
             for u in range(2):
                 t = 2 * h + u
                 if g == 0:
@@ -135,112 +122,137 @@ def tile_picked_zmodd_none_po_kernel(
                     stop=(g == PASSES - 1),
                 )
 
-        def vector_pass(w, g):
-            deal(w, g, on_vector)
-            multiply(w, g, 0)
-            multiply(w, g, 1)
+        def weight_pass(w, g, share=P):
+            for h in range(2):
+                dealt_tile(w, g, h)
+                dst, src = deal_views(w, g, h)
+                on_vector(dst[:, :share], src[:, :share])
+                if share < P:
+                    on_scalar(dst[:, share:], src[:, share:])
+            for h in range(2):
+                multiply(w, g, h)
 
-        def empty(w, t):
+        def empty_y(t, copy):
+            rows[0, t] = tile([P, S], F32, "rows0_%d" % t)
+            copy(rows[0, t][:], banks[0, t][:])
+
+        def empty_mask(w, t):
             rows[w, t] = tile([P, S], F32, "rows%d_%d" % (w, t))
-            on_scalar(rows[w, t][:], banks[w, t][:])
+            nc.scalar.activation(rows[w, t][:], banks[w, t][:], SIGMOID)
 
-        def pick(w, t):
-            picked[w, t] = tile([P, V], F32, "mask%d_%d" % (w, t))
-            nc.scalar.activation(picked[w, t][:], rows[w, t][:].indirect(cen_t[:]), SIGMOID)
+        def scalar_fetch(out, window, offsets):
+            nc.scalar.activation(out, window[:].indirect(offsets), COPY)
 
-        def term(w, t, out):
-            nc.vector.tensor_tensor(out, rows[0, t][:].indirect(pos_t[w][:]), picked[w, t][:], MULT)
+        def vector_fetch(out, window, offsets):
+            on_vector(out, window[:].indirect(offsets))
+
+        def fused_term(out, w, t, sampled):
+            nc.vector.tensor_tensor(out, rows[w, t][:].indirect(cen_t[:]), sampled, MULT)
 
         for g in range(PASSES):
             on_vector(x_codes[g][:], x_table[g][:].bitcast(U32).indirect(offs_t[:]))
         on_vector(x_bytes[:], x_planes[:].indirect(offs_t[:]))
 
-        for w in (1, 0):
-            for g in range(PASSES):
-                vector_pass(w, g)
-        rows[1, 0] = tile([P, S], F32, "rows1_0")
-        nc.scalar.activation(rows[1, 0][:], banks[1, 0][:], SIGMOID)
-        picked[1, 0] = tile([P, V], F32, "mask1_0")
-        on_vector(picked[1, 0][:], rows[1, 0][:].indirect(cen_t[:]))
-        empty(1, 1)
-        empty(1, 2)
-        pick(1, 1)
-        empty(1, 3)
-        pick(1, 2)
-        pick(1, 3)
-
-        vector_pass(2, 0)
+        weight_pass(0, 0, VECTOR_SHARE)
+        weight_pass(0, 1, VECTOR_SHARE)
         for t in range(PACK):
-            empty(0, t)
-        deal(2, 1, on_scalar)
-        early = tile([P, 2, V], F32, "early", "dealt2_0_0")
-        for t in range(2):
-            term(1, t, early[:, t, :])
-        third = tile([P, V], F32, "third", "dealt2_0_1")
-        term(1, 2, third[:])
-        multiply(2, 1, 0, by_tile=True)
-        between = dealt[2, 1, 0][:].rearrange("p u m j -> p (u m j)").bitcast(F32)
-        fourth, fetched = between[:, :V], between[:, V:]
-        term(1, LAST, fourth)
-        on_vector(fetched, rows[0, LAST][:].indirect(pos_t[3][:]))
-        multiply(2, 1, 1)
+            empty_y(t, on_scalar)
 
-        deal_shared(3, 0)
-        multiply(3, 0, 0)
-        multiply(3, 0, 1)
-        vector_pass(3, 1)
-        for t in range(0, PACK, 2):
-            empty(2, t)
-            empty(2, t + 1)
-            pick(2, t)
-            pick(2, t + 1)
-        terms1 = [tile([P, 2, V], F32, "terms1_%d" % h, "dealt3_1_%d" % h) for h in range(2)]
+        y1, y2 = {}, {}
+        y1_all = tile([P, PACK, V], F32, "y1_all")
+        for t in range(1, PACK):
+            y1[t] = y1_all[:, t, :]
+            scalar_fetch(y1[t], rows[0, t], pos1_t[:])
+        for t in range(0, 2):
+            y2[t] = tile([P, V], F32, "y2_%d" % t)[:]
+            scalar_fetch(y2[t], rows[0, t], pos2_t[:])
+
+        weight_pass(1, 0)
+        y1[0] = tile([P, V], F32, "y1_first", "dealt1_0_0")[:]
+        vector_fetch(y1[0], rows[0, 0], pos1_t[:])
+        weight_pass(1, 1)
+
         for t in range(PACK):
-            term(2, t, terms1[t // 2][:, t % 2, :])
-        partial = tile([P, 2, V], F32, "partial")
-        nc.vector.tensor_add(partial[:], early[:], terms1[0][:])
+            empty_mask(1, t)
+        terms1 = {}
+        weight_pass(2, 0)
+        fused1 = tile([P, 1, V], F32, "fused1", "dealt2_0_0")
+        terms1[0] = fused1[:, 0, :]
+        fused_term(terms1[0], 1, 0, y1[0])
+        m1_rest = tile([P, PACK - FUSED1, V], F32, "m1_rest")
+        for t in range(FUSED1, PACK):
+            scalar_fetch(m1_rest[:, t - FUSED1, :], rows[1, t], cen_t[:])
+        y2_rest = tile([P, PACK - 2, V], F32, "y2_rest", "raw2_0")
+        for t in range(2, PACK):
+            y2[t] = y2_rest[:, t - 2, :]
+            scalar_fetch(y2[t], rows[0, t], pos2_t[:])
+        weight_pass(2, 1)
+        late1 = tile([P, PACK - 1, V], F32, "late1", "dealt2_1_0")
+        for t in range(1, PACK):
+            terms1[t] = late1[:, t - 1, :]
+        for t in range(1, FUSED1):
+            fused_term(terms1[t], 1, t, y1[t])
+        nc.vector.tensor_mul(late1[:, FUSED1 - 1 :, :], m1_rest[:], y1_all[:, FUSED1:, :])
+
+        blocks = [(u, slice(a * P, (a + 1) * P)) for u in range(2) for a in range(V // P)]
+
+        def add_turned(bank, pair, first):
+            for n, (u, cols) in enumerate(blocks):
+                nc.tensor.matmul(
+                    bank[:, u, cols], pair[u][:, cols], identity[:],
+                    start=(first and n == 0), stop=(not first and n == len(blocks) - 1), is_transpose=True,
+                )
+
+        turned = [psum.tile([P, 2, V], F32, name="bank") for h in range(2)]
+        for h in range(2):
+            add_turned(turned[h], [terms1[t] for t in (2 * h, 2 * h + 1)], True)
+
+        for t in range(PACK):
+            empty_mask(2, t)
+        weight_pass(3, 0)
+        y3 = tile([P, PACK, V], F32, "y3", "raw3_0")
+        for t in range(PACK):
+            scalar_fetch(y3[:, t, :], rows[0, t], pos3_t[:])
+        weight_pass(3, 1)
+        terms2 = [tile([P, 2, V], F32, "terms2_%d" % h, "dealt3_1_%d" % h) for h in range(2)]
+        for t in range(PACK):
+            fused_term(terms2[t // 2][:, t % 2, :], 2, t, y2[t])
+        for t in range(PACK):
+            empty_mask(3, t)
+
+        def turned_sum(h):
+            add_turned(turned[h], [terms2[h][:, u, :] for u in range(2)], False)
+            staged = tile([P, 2, V], F32, "staged%d" % h)
+            on_scalar(staged[:], turned[h][:])
+            return staged
 
         result = tile([P, PACK, V], F32, "result")
         out_rows = out_0.rearrange("(p t) v -> p t v", t=PACK)
-        for t in range(2):
-            empty(3, t)
-        for t in range(2):
-            pick(3, t)
-        first = tile([P, 2, V], F32, "first", "rows3_1")
-        for t in range(2):
-            term(3, t, first[:, t, :])
-        for t in range(2):
-            nc.vector.tensor_add(result[:, t, :], partial[:, t, :], first[:, t, :])
-        nc.sync.dma_start(out=out_rows[:, :2, :], in_=result[:, :2, :])
+        terms3 = tile([P, PACK, V], F32, "terms3")
 
-        for t in range(2, PACK):
-            empty(3, t)
-        pick(3, 2)
-        turned = psum.tile([P, 2, V], F32, name="bank")
-        blocks = [(u, slice(a * P, (a + 1) * P)) for u in range(2) for a in range(V // P)]
+        staged = turned_sum(0)
+        back = psum.tile([P, 2, V], F32, name="bank")
         for u, cols in blocks:
-            for n, part in enumerate(((third[:], fourth)[u], terms1[1][:, u, :])):
-                nc.tensor.matmul(
-                    turned[:, u, cols], part[:, cols], identity[:], start=(n == 0), stop=(n == 1), is_transpose=True
-                )
-        staged = tile([P, 2, V], F32, "staged")
-        on_scalar(staged[:], turned[:])
-        back = [psum.tile([P, 2, P], F32, name="bank") for a in range(V // P)]
+            nc.tensor.transpose(back[:, u, cols], staged[:, u, cols], identity[:])
+        for t in range(3):
+            fused_term(terms3[:, t, :], 3, t, y3[:, t, :])
+        m3 = tile([P, V], F32, "m3")
+        staged = turned_sum(1)
+        halves = [psum.tile([P, 2, P], F32, name="bank") for a in range(V // P)]
         for a in range(V // P):
             for u in range(2):
-                nc.tensor.transpose(back[a][:, u, :], staged[:, u, a * P : (a + 1) * P], identity[:])
-        second = tile([P, 2, V], F32, "second")
-        term(3, 2, second[:, 0, :])
+                nc.tensor.transpose(halves[a][:, u, :], staged[:, u, a * P : (a + 1) * P], identity[:])
+        nc.vector.tensor_add(result[:, :2, :], back[:], terms3[:, :2, :])
+        nc.sync.dma_start(out=out_rows[:, :2, :], in_=result[:, :2, :])
+
         pieces = [slice(a * V // PIECES, (a + 1) * V // PIECES) for a in range(PIECES)]
-        last_mask = tile([P, V], F32, "last_mask", "dealt3_1_1")
         for cols in pieces:
-            entries = cen_t[:, cols.start // LIST_GROUP : cols.stop // LIST_GROUP]
-            nc.scalar.activation(last_mask[:, cols], rows[3, LAST][:].indirect(entries), SIGMOID)
+            scalar_fetch(m3[:, cols], rows[3, 3], cen_t[:, cols.start // LIST_GROUP : cols.stop // LIST_GROUP])
         for cols in pieces:
-            nc.vector.tensor_mul(second[:, 1, cols], fetched[:, cols], last_mask[:, cols])
+            nc.vector.tensor_mul(terms3[:, 3, cols], m3[:, cols], y3[:, 3, cols])
         for cols in pieces:
             a, begin = divmod(cols.start, P)
-            nc.vector.tensor_add(result[:, 2:, cols], back[a][:, :, begin : begin + V // PIECES], second[:, :, cols])
+            nc.vector.tensor_add(result[:, 2:, cols], halves[a][:, :, begin : begin + V // PIECES], terms3[:, 2:, cols])
         nc.sync.dma_start(out=out_rows[:, 2:, :], in_=result[:, 2:, :])
 
         rounded = tile([P, V, PACK], BF16, "rounded")

@@ -70,17 +70,16 @@ def tile_picked_zmodd_none_po_kernel(
             )
         load_weight(0, 0)
         load_weight(0, 1)
-        pos1_t = load_list(pos1, "pos1_t")
         load_weight(1, 0)
-        pos2_t = load_list(pos2, "pos2_t")
+        pos1_t = load_list(pos1, "pos1_t")
         load_weight(1, 1)
-        cen_t = load_list(cen, "cen_t")
+        pos2_t = load_list(pos2, "pos2_t")
         load_weight(2, 0)
-        load_weight(2, 1)
+        cen_t = load_list(cen, "cen_t")
         pos3_t = load_list(pos3, "pos3_t")
+        load_weight(2, 1)
         load_weight(3, 0)
         load_weight(3, 1)
-        pos_t = {1: pos1_t, 2: pos2_t, 3: pos3_t}
 
         identity = tile([P, P], F32, "identity")
         make_identity(nc, identity[:])
@@ -122,8 +121,8 @@ def tile_picked_zmodd_none_po_kernel(
                     stop=(g == PASSES - 1),
                 )
 
-        def weight_pass(w, g, share=P):
-            for h in range(2):
+        def weight_pass(w, g, shares=(P, P)):
+            for h, share in enumerate(shares):
                 dealt_tile(w, g, h)
                 dst, src = deal_views(w, g, h)
                 on_vector(dst[:, :share], src[:, :share])
@@ -153,17 +152,17 @@ def tile_picked_zmodd_none_po_kernel(
             on_vector(x_codes[g][:], x_table[g][:].bitcast(U32).indirect(offs_t[:]))
         on_vector(x_bytes[:], x_planes[:].indirect(offs_t[:]))
 
-        weight_pass(0, 0, VECTOR_SHARE)
-        weight_pass(0, 1, VECTOR_SHARE)
+        weight_pass(0, 0, (VECTOR_SHARE, VECTOR_SHARE))
+        weight_pass(0, 1, (VECTOR_SHARE, VECTOR_SHARE))
         for t in range(PACK):
             empty_y(t, on_scalar)
 
-        y1, y2 = {}, {}
+        y1, y2, y3, terms1 = {}, {}, {}, {}
         y1_all = tile([P, PACK, V], F32, "y1_all")
         for t in range(1, PACK):
             y1[t] = y1_all[:, t, :]
             scalar_fetch(y1[t], rows[0, t], pos1_t[:])
-        for t in range(0, 2):
+        for t in range(1, 3):
             y2[t] = tile([P, V], F32, "y2_%d" % t)[:]
             scalar_fetch(y2[t], rows[0, t], pos2_t[:])
 
@@ -171,21 +170,23 @@ def tile_picked_zmodd_none_po_kernel(
         y1[0] = tile([P, V], F32, "y1_first", "dealt1_0_0")[:]
         vector_fetch(y1[0], rows[0, 0], pos1_t[:])
         weight_pass(1, 1)
-
+        y2[0] = tile([P, V], F32, "y2_0", "dealt1_1_0")[:]
+        vector_fetch(y2[0], rows[0, 0], pos2_t[:])
         for t in range(PACK):
             empty_mask(1, t)
-        terms1 = {}
         weight_pass(2, 0)
-        fused1 = tile([P, 1, V], F32, "fused1", "dealt2_0_0")
-        terms1[0] = fused1[:, 0, :]
+        terms1[0] = tile([P, V], F32, "fused1", "dealt2_0_0")[:]
         fused_term(terms1[0], 1, 0, y1[0])
         m1_rest = tile([P, PACK - FUSED1, V], F32, "m1_rest")
         for t in range(FUSED1, PACK):
             scalar_fetch(m1_rest[:, t - FUSED1, :], rows[1, t], cen_t[:])
-        y2_rest = tile([P, PACK - 2, V], F32, "y2_rest", "raw2_0")
-        for t in range(2, PACK):
-            y2[t] = y2_rest[:, t - 2, :]
+        middle = tile([P, 3, V], F32, "middle", "raw2_0")
+        for t in range(3, PACK):
+            y2[t] = middle[:, t - 3, :]
             scalar_fetch(y2[t], rows[0, t], pos2_t[:])
+        for t in range(2):
+            y3[t] = middle[:, 1 + t, :]
+            scalar_fetch(y3[t], rows[0, t], pos3_t[:])
         weight_pass(2, 1)
         late1 = tile([P, PACK - 1, V], F32, "late1", "dealt2_1_0")
         for t in range(1, PACK):
@@ -210,14 +211,17 @@ def tile_picked_zmodd_none_po_kernel(
         for t in range(PACK):
             empty_mask(2, t)
         weight_pass(3, 0)
-        y3 = tile([P, PACK, V], F32, "y3", "raw3_0")
-        for t in range(PACK):
-            scalar_fetch(y3[:, t, :], rows[0, t], pos3_t[:])
-        weight_pass(3, 1)
-        terms2 = [tile([P, 2, V], F32, "terms2_%d" % h, "dealt3_1_%d" % h) for h in range(2)]
-        for t in range(PACK):
+        terms2 = []
+        weight_pass(3, 1, (88, 88))
+        y3_late = tile([P, 2, V], F32, "y3_late", "raw3_1")
+        for t in range(2, PACK):
+            y3[t] = y3_late[:, t - 2, :]
+            scalar_fetch(y3[t], rows[0, t], pos3_t[:])
+        for h in range(0, 2):
+            terms2.append(tile([P, 2, V], F32, "terms2_%d" % h, "dealt3_1_%d" % (h - 0)))
+        for t in range(0, PACK):
             fused_term(terms2[t // 2][:, t % 2, :], 2, t, y2[t])
-        for t in range(PACK):
+        for t in range(2):
             empty_mask(3, t)
 
         def turned_sum(h):
@@ -231,11 +235,13 @@ def tile_picked_zmodd_none_po_kernel(
         terms3 = tile([P, PACK, V], F32, "terms3")
 
         staged = turned_sum(0)
+        for t in range(2, PACK):
+            empty_mask(3, t)
         back = psum.tile([P, 2, V], F32, name="bank")
         for u, cols in blocks:
             nc.tensor.transpose(back[:, u, cols], staged[:, u, cols], identity[:])
         for t in range(3):
-            fused_term(terms3[:, t, :], 3, t, y3[:, t, :])
+            fused_term(terms3[:, t, :], 3, t, y3[t])
         m3 = tile([P, V], F32, "m3")
         staged = turned_sum(1)
         halves = [psum.tile([P, 2, P], F32, name="bank") for a in range(V // P)]
@@ -249,7 +255,7 @@ def tile_picked_zmodd_none_po_kernel(
         for cols in pieces:
             scalar_fetch(m3[:, cols], rows[3, 3], cen_t[:, cols.start // LIST_GROUP : cols.stop // LIST_GROUP])
         for cols in pieces:
-            nc.vector.tensor_mul(terms3[:, 3, cols], m3[:, cols], y3[:, 3, cols])
+            nc.vector.tensor_mul(terms3[:, 3, cols], m3[:, cols], y3[3][:, cols])
         for cols in pieces:
             a, begin = divmod(cols.start, P)
             nc.vector.tensor_add(result[:, 2:, cols], halves[a][:, :, begin : begin + V // PIECES], terms3[:, 2:, cols])

from contextlib import ExitStack

import concourse.mybir as mybir
from concourse.masks import make_identity

K, T, S, V, N = 1024, 1024, 512, 256, 512
FLOPS = 4 * 2 * K * N * S

F32 = mybir.dt.float32
BF16 = mybir.dt.bfloat16
I32 = mybir.dt.int32
U32 = mybir.dt.uint32
U16 = mybir.dt.uint16
U8 = mybir.dt.uint8
FP8X4 = mybir.dt.float8_e4m3fn_x4
SIGMOID = mybir.ActivationFunctionType.Sigmoid
COPY = mybir.ActivationFunctionType.Copy
MULT = mybir.AluOpType.mult

P = 128
PACK = 4
K_PASS = P * PACK
PASSES = K // K_PASS
QUADRANT = 32
LIST_GROUP = 16
PIECES = 4
FUSED1 = 2
VECTOR_SHARE = 88


def tile_picked_zmodd_none_po_kernel(
    tc, x_words, x_scales, w0, w1, w2, w3, offs, cen, pos1, pos2, pos3, out_0, out_1, out_2
):
    nc = tc.nc
    weights = (w0, w1, w2, w3)
    on_vector, on_scalar = nc.vector.tensor_copy, nc.scalar.copy
    with ExitStack() as ctx:
        keep = ctx.enter_context(tc.tile_pool(name="keep", bufs=1))
        psum = ctx.enter_context(tc.psum_pool(name="psum", bufs=2 * PACK))

        def tile(shape, dtype, name, tag=None):
            return keep.tile(shape, dtype, name=name, tag=tag or name, align_bytes=64)

        def load_list(src, name):
            offsets = keep.tile([P, src.shape[1]], U16, name=name)
            nc.sync.dma_start(offsets[:], src)
            return offsets

        raw = {}

        def load_weight(w, g):
            raw[w, g] = tile([P, PACK, N], F32, "raw%d_%d" % (w, g))
            k_rows = weights[w][g * K_PASS : (g + 1) * K_PASS, :]
            nc.sync.dma_start(out=raw[w, g][:], in_=k_rows.rearrange("(p j) c -> p j c", j=PACK))

        def load_words(g):
            table = tile([P, T], I32, "x_table%d" % g)
            nc.sync.dma_start(out=table[:], in_=x_words[g].rearrange("p c r -> p (c r)").bitcast(I32))
            return table

        x_planes = tile([P, T], U8, "x_planes")
        nc.vector.memset(x_planes[:].bitcast(I32), 0)
        x_table = [load_words(0)]
        offs_t = load_list(offs, "offs_t")
        x_table.append(load_words(1))
        for q in (0, 2, 1, 3):
            nc.sync.dma_start(
                out=x_planes[QUADRANT * q : QUADRANT * q + PACK * PASSES, :].bitcast(I32),
                in_=x_scales[:, PACK * q : PACK * (q + 1), :].bitcast(I32),
            )
        load_weight(0, 0)
        load_weight(0, 1)
        load_weight(1, 0)
        pos1_t = load_list(pos1, "pos1_t")
        load_weight(1, 1)
        pos2_t = load_list(pos2, "pos2_t")
        load_weight(2, 0)
        cen_t = load_list(cen, "cen_t")
        pos3_t = load_list(pos3, "pos3_t")
        load_weight(2, 1)
        load_weight(3, 0)
        load_weight(3, 1)

        identity = tile([P, P], F32, "identity")
        make_identity(nc, identity[:])
        warm = tile([P, 1], F32, "warm")
        nc.scalar.activation(warm[:], identity[:, 0:1], SIGMOID)

        x_codes = [tile([P, S], U32, "x_codes%d" % g) for g in range(PASSES)]
        x_bytes = tile([P, S], U8, "x_bytes")

        dealt, banks, rows = {}, {}, {}

        def deal_views(w, g, h):
            src = raw[w, g][:].rearrange("p j (m h u) -> p h m j u", h=2, u=2)[:, h]
            return dealt[w, g, h][:].rearrange("p u m j -> p m j u"), src

        def dealt_tile(w, g, h):
            dealt[w, g, h] = tile([P, 2, P, PACK], BF16, "dealt%d_%d_%d" % (w, g, h))

        def multiply(w, g, h):
            codes = tile([P, 2 * P], U32, "codes%d_%d_%d" % (w, g, h))
            scales = tile([P, 2 * P], U8, "scales%d_%d_%d" % (w, g, h))
            nc.vector.quantize_mx(
                out=codes[:].bitcast(FP8X4),
                scales=scales[:],
                in_=dealt[w, g, h][:].rearrange("p u m j -> p (u m j)"),
            )
            for u in range(2):
                t = 2 * h + u
                if g == 0:
                    banks[w, t] = psum.tile([P, S], F32, name="bank")
                cols = slice(u * P, (u + 1) * P)
                nc.tensor.matmul_mx(
                    out=banks[w, t][:],
                    lhsT=codes[:, cols].bitcast(FP8X4),
                    lhsT_scale=scales[:, cols],
                    rhs=x_codes[g][:].bitcast(FP8X4),
                    rhs_scale=x_bytes[PACK * g :, :],
                    start=(g == 0),
                    stop=(g == PASSES - 1),
                )

        def weight_pass(w, g, shares=(P, P)):
            for h, share in enumerate(shares):
                dealt_tile(w, g, h)
                dst, src = deal_views(w, g, h)
                on_vector(dst[:, :share], src[:, :share])
                if share < P:
                    on_scalar(dst[:, share:], src[:, share:])
            for h in range(2):
                multiply(w, g, h)

        def empty_y(t, copy):
            rows[0, t] = tile([P, S], F32, "rows0_%d" % t)
            copy(rows[0, t][:], banks[0, t][:])

        def empty_mask(w, t):
            rows[w, t] = tile([P, S], F32, "rows%d_%d" % (w, t))
            nc.scalar.activation(rows[w, t][:], banks[w, t][:], SIGMOID)

        def scalar_fetch(out, window, offsets):
            nc.scalar.activation(out, window[:].indirect(offsets), COPY)

        def vector_fetch(out, window, offsets):
            on_vector(out, window[:].indirect(offsets))

        def fused_term(out, w, t, sampled):
            nc.vector.tensor_tensor(out, rows[w, t][:].indirect(cen_t[:]), sampled, MULT)

        for g in range(PASSES):
            on_vector(x_codes[g][:], x_table[g][:].bitcast(U32).indirect(offs_t[:]))
        on_vector(x_bytes[:], x_planes[:].indirect(offs_t[:]))

        weight_pass(0, 0, (VECTOR_SHARE, VECTOR_SHARE))
        weight_pass(0, 1, (VECTOR_SHARE, VECTOR_SHARE))
        for t in range(PACK):
            empty_y(t, on_scalar)

        y1, y2, y3, terms1 = {}, {}, {}, {}
        y1_all = tile([P, PACK, V], F32, "y1_all")
        for t in range(1, PACK):
            y1[t] = y1_all[:, t, :]
            scalar_fetch(y1[t], rows[0, t], pos1_t[:])
        for t in range(1, 3):
            y2[t] = tile([P, V], F32, "y2_%d" % t)[:]
            scalar_fetch(y2[t], rows[0, t], pos2_t[:])

        weight_pass(1, 0)
        y1[0] = tile([P, V], F32, "y1_first", "dealt1_0_0")[:]
        vector_fetch(y1[0], rows[0, 0], pos1_t[:])
        weight_pass(1, 1)
        y2[0] = tile([P, V], F32, "y2_0", "dealt1_1_0")[:]
        vector_fetch(y2[0], rows[0, 0], pos2_t[:])
        for t in range(PACK):
            empty_mask(1, t)
        weight_pass(2, 0)
        terms1[0] = tile([P, V], F32, "fused1", "dealt2_0_0")[:]
        fused_term(terms1[0], 1, 0, y1[0])
        m1_rest = tile([P, PACK - FUSED1, V], F32, "m1_rest")
        for t in range(FUSED1, PACK):
            scalar_fetch(m1_rest[:, t - FUSED1, :], rows[1, t], cen_t[:])
        middle = tile([P, 3, V], F32, "middle", "raw2_0")
        for t in range(3, PACK):
            y2[t] = middle[:, t - 3, :]
            scalar_fetch(y2[t], rows[0, t], pos2_t[:])
        for t in range(2):
            y3[t] = middle[:, 1 + t, :]
            scalar_fetch(y3[t], rows[0, t], pos3_t[:])
        weight_pass(2, 1)
        late1 = tile([P, PACK - 1, V], F32, "late1", "dealt2_1_0")
        for t in range(1, PACK):
            terms1[t] = late1[:, t - 1, :]
        for t in range(1, FUSED1):
            fused_term(terms1[t], 1, t, y1[t])
        nc.vector.tensor_mul(late1[:, FUSED1 - 1 :, :], m1_rest[:], y1_all[:, FUSED1:, :])

        blocks = [(u, slice(a * P, (a + 1) * P)) for u in range(2) for a in range(V // P)]

        def add_turned(bank, pair, first):
            for n, (u, cols) in enumerate(blocks):
                nc.tensor.matmul(
                    bank[:, u, cols], pair[u][:, cols], identity[:],
                    start=(first and n == 0), stop=(not first and n == len(blocks) - 1), is_transpose=True,
                )

        turned = [psum.tile([P, 2, V], F32, name="bank") for h in range(2)]
        for h in range(2):
            add_turned(turned[h], [terms1[t] for t in (2 * h, 2 * h + 1)], True)

        for t in range(PACK):
            empty_mask(2, t)
        weight_pass(3, 0)
        terms2 = []
        weight_pass(3, 1, (88, 88))
        y3_late = tile([P, 2, V], F32, "y3_late", "raw3_1")
        for t in range(2, PACK):
            y3[t] = y3_late[:, t - 2, :]
            scalar_fetch(y3[t], rows[0, t], pos3_t[:])
        for h in range(0, 2):
            terms2.append(tile([P, 2, V], F32, "terms2_%d" % h, "dealt3_1_%d" % (h - 0)))
        for t in range(0, PACK):
            fused_term(terms2[t // 2][:, t % 2, :], 2, t, y2[t])
        for t in range(2):
            empty_mask(3, t)

        def turned_sum(h):
            add_turned(turned[h], [terms2[h][:, u, :] for u in range(2)], False)
            staged = tile([P, 2, V], F32, "staged%d" % h)
            on_scalar(staged[:], turned[h][:])
            return staged

        result = tile([P, PACK, V], F32, "result")
        out_rows = out_0.rearrange("(p t) v -> p t v", t=PACK)
        terms3 = tile([P, PACK, V], F32, "terms3")

        staged = turned_sum(0)
        for t in range(2, PACK):
            empty_mask(3, t)
        back = psum.tile([P, 2, V], F32, name="bank")
        for u, cols in blocks:
            nc.tensor.transpose(back[:, u, cols], staged[:, u, cols], identity[:])
        for t in range(3):
            fused_term(terms3[:, t, :], 3, t, y3[t])
        m3 = tile([P, V], F32, "m3")
        staged = turned_sum(1)
        halves = [psum.tile([P, 2, P], F32, name="bank") for a in range(V // P)]
        for a in range(V // P):
            for u in range(2):
                nc.tensor.transpose(halves[a][:, u, :], staged[:, u, a * P : (a + 1) * P], identity[:])
        nc.vector.tensor_add(result[:, :2, :], back[:], terms3[:, :2, :])
        nc.sync.dma_start(out=out_rows[:, :2, :], in_=result[:, :2, :])

        pieces = [slice(a * V // PIECES, (a + 1) * V // PIECES) for a in range(PIECES)]
        for cols in pieces:
            scalar_fetch(m3[:, cols], rows[3, 3], cen_t[:, cols.start // LIST_GROUP : cols.stop // LIST_GROUP])
        for cols in pieces:
            nc.vector.tensor_mul(terms3[:, 3, cols], m3[:, cols], y3[3][:, cols])
        for cols in pieces:
            a, begin = divmod(cols.start, P)
            nc.vector.tensor_add(result[:, 2:, cols], halves[a][:, :, begin : begin + V // PIECES], terms3[:, 2:, cols])
        nc.sync.dma_start(out=out_rows[:, 2:, :], in_=result[:, 2:, :])

        rounded = tile([P, V, PACK], BF16, "rounded")
        for n, cols in enumerate(pieces):
            copy = on_scalar if n == 0 else on_vector
            copy(
                rounded[:, cols, :].rearrange("p (c i) t -> p c t i", i=PACK),
                result[:, :, cols].rearrange("p t (c i) -> p c t i", i=PACK),
            )
        out_codes = tile([P, V], U32, "out_codes")
        out_scales = tile([P, V], U8, "out_scales")
        for cols in pieces:
            nc.vector.quantize_mx(
                out=out_codes[:, cols].bitcast(FP8X4),
                scales=out_scales[:, cols],
                in_=rounded[:, cols, :].rearrange("p v t -> p (v t)"),
            )
        nc.sync.dma_start(out=out_1[0].rearrange("p c r -> p (c r)").bitcast(I32), in_=out_codes[:].bitcast(I32))
        for q in range(P // QUADRANT):
            queue = nc.scalar if q % 2 else nc.sync
            queue.dma_start(
                out=out_2[0, PACK * q : PACK * (q + 1), :].bitcast(I32),
                in_=out_scales[QUADRANT * q : QUADRANT * q + PACK, :].bitcast(I32),
            )
